import numpy as np
import ml_dtypes


def mxq(x, axis, fmt="e4m3"):
    dtype, down = {"e4m3": (ml_dtypes.float8_e4m3fn, 7), "e5m2": (ml_dtypes.float8_e5m2, 14)}[fmt]
    v = np.moveaxis(np.asarray(x, np.float32).astype(ml_dtypes.bfloat16).astype(np.float64), axis, -1)
    blocks = v.reshape(v.shape[:-1] + (-1, 32))
    amax = np.abs(blocks).max(-1, keepdims=True)
    byte = np.maximum(np.where(amax > 0, np.frexp(amax)[1] - 1 + 127, 0) - down, 1)
    scale = np.exp2(byte - 127.0)
    codes = (blocks / scale).astype(np.float32).astype(dtype).astype(np.float64)
    return np.moveaxis((codes * scale).reshape(v.shape), -1, axis)


WIDE = False


def mx_kscale(k):
    if not WIDE:
        return np.ones(k)
    levels = np.array([10, -10, 5, -5, 0])
    if k % 512:
        return np.exp2(np.random.permutation(np.resize(levels, k // 32))).repeat(32)
    a = np.empty((k // 512, 16))
    for p in range(k // 512):
        a[p, :8] = np.random.permutation(np.resize(levels, 8))
        for g in range(8):
            far = levels[np.abs(levels - a[p, g]) >= 10]
            a[p, g + 8] = far[np.random.randint(len(far))]
    return np.exp2(a.ravel()).repeat(32)


def f64(x):
    return np.asarray(x).astype(np.float64)


def striped(idx):
    return np.tile(idx.reshape(-1, 16).T, (8, 1)).astype(np.uint16)


def unstriped(offs):
    return offs[:16].T.reshape(-1).astype(np.int64)


E2M1 = np.array([0.0, 0.5, 1.0, 1.5, 2.0, 3.0, 4.0, 6.0, -0.0, -0.5, -1.0, -1.5, -2.0, -3.0, -4.0, -6.0])


def pack_weight(w, fmt):
    k, n = w.shape
    w = f64(np.asarray(w, np.float32).astype(ml_dtypes.bfloat16)).reshape(k // 32, 32, n)
    amax = np.abs(w).max(1)
    if fmt == "e4m3":
        byte = np.frexp(amax)[1] - 1 + 127 - 7
    else:
        mant, ex = np.frexp(amax / 6.0)
        byte = np.where(mant > 0.5, ex, ex - 1) + 127
    byte = np.clip(np.where(amax > 0, byte, 1), 1, 254)
    scaled = (w * np.exp2(127.0 - byte)[:, None, :]).reshape(k, n).astype(np.float32)
    by_word = np.ascontiguousarray(scaled.reshape(k // 512, 128, 4, n).transpose(0, 1, 3, 2))
    if fmt == "e4m3":
        words = by_word.astype(ml_dtypes.float8_e4m3fn).view(np.uint8)
    else:
        c = by_word.astype(ml_dtypes.float4_e2m1fn).view(np.uint8) & 0xF
        words = (c[..., 0::2] | (c[..., 1::2] << 4)).reshape(k // 512, 128, 2 * n)
    return np.ascontiguousarray(words), np.ascontiguousarray(byte.astype(np.uint8).reshape(k // 512, 16, n))


def unpack_weight(words, scales, fmt):
    g, _, n = scales.shape
    words = np.ascontiguousarray(words).reshape(g, 128, n, -1)
    if fmt == "e4m3":
        vals = words.view(ml_dtypes.float8_e4m3fn).astype(np.float64)
    else:
        nib = np.empty((g, 128, n, 4), np.uint8)
        nib[..., 0::2] = words & 0xF
        nib[..., 1::2] = words >> 4
        vals = E2M1[nib]
    vals = vals * np.repeat(np.exp2(scales.astype(np.float64) - 127.0), 8, axis=1)[..., None]
    return vals.transpose(0, 1, 3, 2).reshape(g * 512, n)


def gelu(v):
    return 0.5 * v * (1.0 + np.tanh(np.sqrt(2.0 / np.pi) * (v + 0.044715 * v**3)))


K, T, S, H, N = 1536, 2048, 1024, 512, 256

def setup_inputs():
    n = np.random.standard_normal
    s = mx_kscale(K)[:, None]
    u = mx_kscale(H)[:, None]
    tab_words, tab_scales = pack_weight(n((K, T)) * s, "e4m3")
    w1 = (n((K, H)) / np.sqrt(K) / s).astype(np.float32)
    w2_words, w2_scales = pack_weight(n((K, H)) / np.sqrt(K) / s, "e2m1")
    gT = (np.exp(0.5 * n((H, T))) * u).astype(np.float32)
    w3 = (n((H, N)) / np.sqrt(H) / u).astype(np.float32)
    offs = striped(np.random.permutation(T)[:S])
    return {"tab_words": tab_words, "tab_scales": tab_scales, "offs": offs, "w1": w1,
            "w2_words": w2_words, "w2_scales": w2_scales, "gT": gT, "w3": w3}

def reference(tab_words, tab_scales, offs, w1, w2_words, w2_scales, gT, w3):
    v = unpack_weight(tab_words, tab_scales, "e4m3")[:, unstriped(offs)]
    g = f64(gT)[:, unstriped(offs)]
    w1q = mxq(f64(w1), 0, "e4m3")
    w2q = unpack_weight(w2_words, w2_scales, "e2m1")
    a = w1q.T @ v
    b = w2q.T @ v
    h = np.square(np.tanh(a) - np.tanh(b)) * g
    hq = mxq(h, 0, "e4m3")
    w3q = mxq(f64(w3), 0, "e4m3")
    return w3q.T @ hq

@@ -1,0 +1,260 @@
+from contextlib import ExitStack
+
+import concourse.mybir as mybir
+
+K, T, S, H, N = 1536, 2048, 1024, 512, 256
+FLOPS = 2 * (2 * K * H * S + H * N * S)
+
+F32 = mybir.dt.float32
+BF16 = mybir.dt.bfloat16
+I32 = mybir.dt.int32
+U32 = mybir.dt.uint32
+U16 = mybir.dt.uint16
+U8 = mybir.dt.uint8
+FP8X4 = mybir.dt.float8_e4m3fn_x4
+FP4X4 = mybir.dt.float4_e2m1fn_x4
+ACT = mybir.ActivationFunctionType
+ALU = mybir.AluOpType
+
+P = 128
+PACK = 4
+PASSES = K // (P * PACK)
+HALF = S // 2
+MOVED_ROWS = 112
+
+
+def tile_list_crystal_disagreement_scores_kernel(
+    tc, tab_words, tab_scales, offs, w1, w2_words, w2_scales, gT, w3, out
+):
+    nc = tc.nc
+    with ExitStack() as ctx:
+        keep = ctx.enter_context(tc.tile_pool(name="keep", bufs=1))
+        ring = ctx.enter_context(tc.tile_pool(name="ring", bufs=4))
+        psum = ctx.enter_context(tc.psum_pool(name="psum", bufs=8))
+
+        offsets = keep.tile([P, S // 16], U16, name="offsets")
+        tab, w1_raw, g_tab = {}, {}, {}
+        tab_sc = keep.tile([P, T // 4], I32, name="tab_sc")
+        w2_raw = keep.tile([P, PASSES, H // 2], I32, name="w2_raw")
+        w2_sc_raw = keep.tile([P, PASSES, H // 4], I32, name="w2_sc_raw")
+
+        v = [keep.tile([P, S], U32, name=f"v{a}", align_bytes=64) for a in range(PASSES)]
+        v_sc0 = keep.tile([P, S], U8, name="v_sc0", align_bytes=64)
+        v_sc_moved = [keep.tile([P, S // 4], I32, name=f"v_sc_moved{a}", align_bytes=64) for a in range(1, PASSES)]
+        w2q = keep.tile([P, PASSES, 2 * H], U8, name="w2q", align_bytes=64)
+        w2_sc = keep.tile([P, PASSES, H], U8, name="w2_sc", align_bytes=64)
+        w1_bf = [keep.tile([P, PACK * H], BF16, name=f"w1_bf{a}", align_bytes=64) for a in range(PASSES)]
+        w1q = [keep.tile([P, H], U32, name=f"w1q{a}", align_bytes=64) for a in range(PASSES)]
+        w1_sc = [keep.tile([P, H], U8, name=f"w1_sc{a}", align_bytes=64) for a in range(PASSES)]
+        w3_bf = keep.tile([P, PACK * N], BF16, name="w3_bf", align_bytes=64)
+        w3q = keep.tile([P, N], U32, name="w3q", align_bytes=64)
+        w3_sc = keep.tile([P, N], U8, name="w3_sc", align_bytes=64)
+        tanh_b = keep.tile([P, PACK, S], F32, name="tanh_b")
+        sq = {}
+        h_f32 = keep.tile([P, PACK, S], F32, name="h_f32")
+        h_bf = keep.tile([P, S * PACK], BF16, name="h_bf", align_bytes=64)
+        hq = keep.tile([P, S], U32, name="hq", align_bytes=64)
+        h_sc = keep.tile([P, S], U8, name="h_sc", align_bytes=64)
+
+        def listed(lo, hi):
+            return offsets[:, lo // 16 : hi // 16]
+
+        def load_tab(a):
+            tab.setdefault(a, keep.tile([P, T], I32, name=f"tab{a}"))
+            nc.sync.dma_start(tab[a][:], tab_words[a].rearrange("p n i -> p (n i)").bitcast(I32))
+
+        def load_w1(a):
+            w1_raw.setdefault(a, keep.tile([P, PACK, H], F32, name=f"w1_raw{a}"))
+            rows = w1[a * P * PACK : (a + 1) * P * PACK, :]
+            nc.sync.dma_start(w1_raw[a][:], rows.rearrange("(p j) c -> p j c", j=PACK))
+
+        nc.sync.dma_start(offsets[:], offs)
+        nc.gpsimd.memset(tab_sc[:], 0)
+        for q in range(4):
+            nc.scalar.dma_start(
+                tab_sc[32 * q : 32 * q + 4 * PASSES, :], tab_scales[:, 4 * q : 4 * q + 4, :].bitcast(I32)
+            )
+        nc.sync.dma_start(w2_raw[:], w2_words.rearrange("a p c -> p a c").bitcast(I32))
+        load_tab(0)
+        load_tab(1)
+        nc.gpsimd.memset(w2_sc_raw[:], 0)
+        for q in range(4):
+            nc.gpsimd.dma_start(
+                w2_sc_raw[32 * q : 32 * q + 4, :, :],
+                w2_scales[:, 4 * q : 4 * q + 4, :].rearrange("a r c -> r a c").bitcast(I32),
+            )
+        for moved in v_sc_moved:
+            nc.vector.memset(moved[:], 0)
+        load_w1(0)
+        load_tab(2)
+        load_w1(1)
+        load_w1(2)
+        g_rows = gT.rearrange("(p t) n -> p t n", t=PACK)
+        w3_raw = keep.tile([P, PACK, N], F32, name="w3_raw")
+        for t in range(PACK):
+            g_tab.setdefault(t, keep.tile([P, T], F32, name=f"g_tab{t}"))
+            nc.sync.dma_start(g_tab[t][:], g_rows[:, t, :])
+            if t == 1:
+                nc.sync.dma_start(w3_raw[:], w3.rearrange("(p j) c -> p j c", j=PACK))
+
+        nc.vector.tensor_copy(
+            w2q[:].bitcast(U16).rearrange("p a (t m) -> p t a m", t=PACK),
+            w2_raw[:].bitcast(U16).rearrange("p a (m t) -> p t a m", t=PACK),
+        )
+        nc.vector.tensor_copy(v_sc0[:], tab_sc[:].bitcast(U8).indirect(offsets[:]))
+        for a in range(1, PASSES):
+            nc.scalar.dma_start(
+                v_sc_moved[a - 1][0:MOVED_ROWS, :], v_sc0[4 * a : 4 * a + MOVED_ROWS, :].bitcast(I32)
+            )
+        v_sc = [v_sc0[:]] + [moved[:].bitcast(U8) for moved in v_sc_moved]
+
+        def gather_words(a, lo, hi):
+            nc.vector.tensor_copy(v[a][:, lo:hi], tab[a][:].bitcast(U32).indirect(listed(lo, hi)))
+
+        def interleave_w1(engine_copy, a, t0, t1):
+            engine_copy(
+                w1_bf[a][:].rearrange("p (t m j) -> p m j t", t=PACK, j=PACK)[:, :, :, t0:t1],
+                w1_raw[a][:].rearrange("p j (m t) -> p m j t", t=PACK)[:, :, :, t0:t1],
+            )
+
+        def quantize_w1(a, t0, t1):
+            nc.vector.quantize_mx(
+                out=w1q[a][:, t0 * P : t1 * P].bitcast(FP8X4),
+                scales=w1_sc[a][:, t0 * P : t1 * P],
+                in_=w1_bf[a][:, t0 * P * PACK : t1 * P * PACK],
+            )
+
+        gather_words(0, 0, S)
+        nc.vector.tensor_copy(
+            w2_sc[:].rearrange("p a (t m) -> p t a m", t=PACK),
+            w2_sc_raw[:].bitcast(U8).rearrange("p a (m t) -> p t a m", t=PACK),
+        )
+        gather_words(1, 0, S)
+        interleave_w1(nc.scalar.copy, 0, 0, PACK)
+        gather_words(2, 0, HALF)
+        gather_words(2, HALF, S)
+        quantize_w1(0, 0, PACK)
+
+        units = [(0, 0), (0, 1), (1, 0), (2, 0), (3, 0), (1, 1), (2, 1), (3, 1)]
+
+        def head_pass(bank, lhsT, lhsT_scale, a, half):
+            cols = slice(half * HALF, (half + 1) * HALF)
+            nc.tensor.matmul_mx(
+                out=bank[:],
+                lhsT=lhsT,
+                lhsT_scale=lhsT_scale,
+                rhs=v[a][:, cols].bitcast(FP8X4),
+                rhs_scale=v_sc[a][:, cols],
+                start=(a == 0),
+                stop=(a == PASSES - 1),
+            )
+
+        b_banks = [psum.tile([P, HALF], F32, name="bank") for u in units]
+
+        def b_pass(u, a):
+            t, half = units[u]
+            head_pass(
+                b_banks[u],
+                w2q[:, a, 2 * t * P : 2 * (t + 1) * P].bitcast(FP4X4),
+                w2_sc[:, a, t * P : (t + 1) * P],
+                a,
+                half,
+            )
+
+        def b_tanh(u):
+            t, half = units[u]
+            nc.scalar.activation(tanh_b[:, t, half * HALF : (half + 1) * HALF], b_banks[u][:], ACT.Tanh)
+
+        for a in range(PASSES):
+            for u in range(len(units)):
+                b_pass(u, a)
+        interleave_w1(nc.scalar.copy, 1, 0, PACK)
+        interleave_w1(nc.vector.tensor_copy, 2, 0, 2)
+        quantize_w1(1, 0, PACK)
+        quantize_w1(2, 0, 2)
+        interleave_w1(nc.vector.tensor_copy, 2, 2, PACK)
+        quantize_w1(2, 2, PACK)
+
+        def squared_difference(t, half):
+            cols = slice(half * HALF, (half + 1) * HALF)
+            bank = psum.tile([P, HALF], F32, name="bank")
+            for a in range(PASSES):
+                head_pass(
+                    bank, w1q[a][:, t * P : (t + 1) * P].bitcast(FP8X4), w1_sc[a][:, t * P : (t + 1) * P], a, half
+                )
+            tanh_a = ring.tile([P, HALF], F32, name="tanh_a")
+            nc.scalar.activation(tanh_a[:], bank[:], ACT.Tanh)
+            diff = ring.tile([P, HALF], F32, name="diff", bufs=2)
+            nc.vector.tensor_tensor(diff[:], tanh_a[:], tanh_b[:, t, cols], ALU.subtract)
+            sq.setdefault((t, half), ring.tile([P, HALF], F32, name="sq", bufs=3))
+            nc.scalar.activation(sq[t, half][:], diff[:], ACT.Square)
+
+        def weigh(t, lo, hi):
+            half, start = divmod(lo, HALF)
+            nc.vector.tensor_tensor(
+                h_f32[:, t, lo:hi],
+                g_tab[t][:].indirect(listed(lo, hi)),
+                sq[t, half][:, start : start + hi - lo],
+                ALU.mult,
+            )
+
+        def interleave_h(engine_copy, lo, hi):
+            engine_copy(
+                h_bf[:, lo * PACK : hi * PACK].rearrange("p (c i t) -> p c t i", i=4, t=PACK),
+                h_f32[:, :, lo:hi].rearrange("p t (c i) -> p c t i", i=4),
+            )
+
+        out_view = out.rearrange("(b p) j -> p b j", p=P)
+
+        def read_out(lo, hi):
+            nc.vector.quantize_mx(
+                out=hq[:, lo:hi].bitcast(FP8X4), scales=h_sc[:, lo:hi], in_=h_bf[:, lo * PACK : hi * PACK]
+            )
+            for c0 in range(lo, hi, 256):
+                bank = psum.tile([P, 2, 256], F32, name="bank")
+                for b in range(N // P):
+                    nc.tensor.matmul_mx(
+                        out=bank[:, b, :],
+                        lhsT=w3q[:, b * P : (b + 1) * P].bitcast(FP8X4),
+                        lhsT_scale=w3_sc[:, b * P : (b + 1) * P],
+                        rhs=hq[:, c0 : c0 + 256].bitcast(FP8X4),
+                        rhs_scale=h_sc[:, c0 : c0 + 256],
+                        start=True,
+                        stop=True,
+                    )
+                res = ring.tile([P, 2, 256], F32, name="res")
+                nc.scalar.copy(res[:], bank[:])
+                nc.sync.dma_start(out_view[:, :, c0 : c0 + 256], res[:])
+
+        b_tanh(0)
+        b_tanh(1)
+        b_tanh(2)
+        squared_difference(*units[0])
+        for u in range(1, 5):
+            b_tanh(u + 2)
+            squared_difference(*units[u])
+            t, half = units[u - 1]
+            weigh(t, half * HALF, (half + 1) * HALF)
+        b_tanh(7)
+        squared_difference(*units[5])
+        weigh(3, 0, HALF)
+        squared_difference(*units[6])
+        squared_difference(*units[7])
+        nc.scalar.copy(
+            w3_bf[:].rearrange("p (c i j) -> p c j i", i=4, j=PACK),
+            w3_raw[:].rearrange("p j (c i) -> p c j i", i=4),
+        )
+        interleave_h(nc.scalar.copy, 0, 256)
+        interleave_h(nc.scalar.copy, 256, HALF)
+        weigh(1, HALF, S)
+        nc.vector.quantize_mx(out=w3q[:].bitcast(FP8X4), scales=w3_sc[:], in_=w3_bf[:])
+        weigh(2, HALF, 768)
+        weigh(3, HALF, 768)
+        interleave_h(nc.scalar.copy, HALF, 768)
+        read_out(0, 256)
+        weigh(2, 768, S)
+        read_out(256, HALF)
+        weigh(3, 768, S)
+        interleave_h(nc.vector.tensor_copy, 768, S)
+        read_out(HALF, 768)
+        read_out(768, S)

@@ -30,7 +30,7 @@ def tile_list_crystal_disagreement_scores_kernel(
     with ExitStack() as ctx:
         keep = ctx.enter_context(tc.tile_pool(name="keep", bufs=1))
         ring = ctx.enter_context(tc.tile_pool(name="ring", bufs=4))
-        psum = ctx.enter_context(tc.psum_pool(name="psum", bufs=8))
+        psum = ctx.enter_context(tc.psum_pool(name="psum", bufs=1))
 
         offsets = keep.tile([P, S // 16], U16, name="offsets")
         tab, w1_raw, g_tab = {}, {}, {}
@@ -68,46 +68,6 @@ def tile_list_crystal_disagreement_scores_kernel(
             rows = w1[a * P * PACK : (a + 1) * P * PACK, :]
             nc.sync.dma_start(w1_raw[a][:], rows.rearrange("(p j) c -> p j c", j=PACK))
 
-        nc.sync.dma_start(offsets[:], offs)
-        nc.gpsimd.memset(tab_sc[:], 0)
-        for q in range(4):
-            nc.scalar.dma_start(
-                tab_sc[32 * q : 32 * q + 4 * PASSES, :], tab_scales[:, 4 * q : 4 * q + 4, :].bitcast(I32)
-            )
-        nc.sync.dma_start(w2_raw[:], w2_words.rearrange("a p c -> p a c").bitcast(I32))
-        load_tab(0)
-        load_tab(1)
-        nc.gpsimd.memset(w2_sc_raw[:], 0)
-        for q in range(4):
-            nc.gpsimd.dma_start(
-                w2_sc_raw[32 * q : 32 * q + 4, :, :],
-                w2_scales[:, 4 * q : 4 * q + 4, :].rearrange("a r c -> r a c").bitcast(I32),
-            )
-        for moved in v_sc_moved:
-            nc.vector.memset(moved[:], 0)
-        load_w1(0)
-        load_tab(2)
-        load_w1(1)
-        load_w1(2)
-        g_rows = gT.rearrange("(p t) n -> p t n", t=PACK)
-        w3_raw = keep.tile([P, PACK, N], F32, name="w3_raw")
-        for t in range(PACK):
-            g_tab.setdefault(t, keep.tile([P, T], F32, name=f"g_tab{t}"))
-            nc.sync.dma_start(g_tab[t][:], g_rows[:, t, :])
-            if t == 1:
-                nc.sync.dma_start(w3_raw[:], w3.rearrange("(p j) c -> p j c", j=PACK))
-
-        nc.vector.tensor_copy(
-            w2q[:].bitcast(U16).rearrange("p a (t m) -> p t a m", t=PACK),
-            w2_raw[:].bitcast(U16).rearrange("p a (m t) -> p t a m", t=PACK),
-        )
-        nc.vector.tensor_copy(v_sc0[:], tab_sc[:].bitcast(U8).indirect(offsets[:]))
-        for a in range(1, PASSES):
-            nc.scalar.dma_start(
-                v_sc_moved[a - 1][0:MOVED_ROWS, :], v_sc0[4 * a : 4 * a + MOVED_ROWS, :].bitcast(I32)
-            )
-        v_sc = [v_sc0[:]] + [moved[:].bitcast(U8) for moved in v_sc_moved]
-
         def gather_words(a, lo, hi):
             nc.vector.tensor_copy(v[a][:, lo:hi], tab[a][:].bitcast(U32).indirect(listed(lo, hi)))
 
@@ -124,7 +84,48 @@ def tile_list_crystal_disagreement_scores_kernel(
                 in_=w1_bf[a][:, t0 * P * PACK : t1 * P * PACK],
             )
 
+        nc.gpsimd.memset(tab_sc[:], 0)
+        nc.gpsimd.memset(w2_sc_raw[:], 0)
+        for moved in v_sc_moved:
+            nc.vector.memset(moved[:], 0)
+        nc.sync.dma_start(offsets[:], offs)
+        load_tab(0)
+        for q in range(4):
+            nc.sync.dma_start(
+                tab_sc[32 * q : 32 * q + 4 * PASSES, :], tab_scales[:, 4 * q : 4 * q + 4, :].bitcast(I32)
+            )
+        nc.sync.dma_start(w2_raw[:], w2_words.rearrange("a p c -> p a c").bitcast(I32))
+        for q in range(4):
+            nc.sync.dma_start(
+                w2_sc_raw[32 * q : 32 * q + 4, :, :],
+                w2_scales[:, 4 * q : 4 * q + 4, :].rearrange("a r c -> r a c").bitcast(I32),
+            )
+        load_tab(1)
+        load_tab(2)
+        load_w1(0)
+
         gather_words(0, 0, S)
+        nc.vector.tensor_copy(v_sc0[:], tab_sc[:].bitcast(U8).indirect(offsets[:]))
+        for a in range(1, PASSES):
+            nc.sync.dma_start(
+                v_sc_moved[a - 1][0:MOVED_ROWS, :], v_sc0[4 * a : 4 * a + MOVED_ROWS, :].bitcast(I32)
+            )
+        v_sc = [v_sc0[:]] + [moved[:].bitcast(U8) for moved in v_sc_moved]
+
+        load_w1(1)
+        load_w1(2)
+        g_rows = gT.rearrange("(p t) n -> p t n", t=PACK)
+        w3_raw = keep.tile([P, PACK, N], F32, name="w3_raw")
+        for t in range(PACK):
+            g_tab.setdefault(t, keep.tile([P, T], F32, name=f"g_tab{t}"))
+            nc.sync.dma_start(g_tab[t][:], g_rows[:, t, :])
+            if t == 0:
+                nc.sync.dma_start(w3_raw[:], w3.rearrange("(p j) c -> p j c", j=PACK))
+
+        nc.vector.tensor_copy(
+            w2q[:].bitcast(U16).rearrange("p a (t m) -> p t a m", t=PACK),
+            w2_raw[:].bitcast(U16).rearrange("p a (m t) -> p t a m", t=PACK),
+        )
         nc.vector.tensor_copy(
             w2_sc[:].rearrange("p a (t m) -> p t a m", t=PACK),
             w2_sc_raw[:].bitcast(U8).rearrange("p a (m t) -> p t a m", t=PACK),
@@ -149,7 +150,10 @@ def tile_list_crystal_disagreement_scores_kernel(
                 stop=(a == PASSES - 1),
             )
 
-        b_banks = [psum.tile([P, HALF], F32, name="bank") for u in units]
+        b_bank_of = [0,1,2,3,4,6,5,7]
+        a_bank_of = [5,6,7,5,7,6,5,6]
+        banks = [psum.tile([P, HALF], F32, name=f"bank{i}") for i in range(8)]
+        b_banks = [banks[i] for i in b_bank_of]
 
         def b_pass(u, a):
             t, half = units[u]
@@ -163,21 +167,21 @@ def tile_list_crystal_disagreement_scores_kernel(
 
         def b_tanh(u):
             t, half = units[u]
+            for a in range(PASSES):
+                b_pass(u, a)
             nc.scalar.activation(tanh_b[:, t, half * HALF : (half + 1) * HALF], b_banks[u][:], ACT.Tanh)
 
-        for a in range(PASSES):
-            for u in range(len(units)):
-                b_pass(u, a)
-        interleave_w1(nc.scalar.copy, 1, 0, PACK)
-        interleave_w1(nc.vector.tensor_copy, 2, 0, 2)
+        interleave_w1(nc.vector.tensor_copy, 1, 0, PACK)
         quantize_w1(1, 0, PACK)
+        interleave_w1(nc.vector.tensor_copy, 2, 0, 2)
         quantize_w1(2, 0, 2)
-        interleave_w1(nc.vector.tensor_copy, 2, 2, PACK)
+        interleave_w1(nc.scalar.copy, 2, 2, PACK)
         quantize_w1(2, 2, PACK)
 
         def squared_difference(t, half):
             cols = slice(half * HALF, (half + 1) * HALF)
-            bank = psum.tile([P, HALF], F32, name="bank")
+            u = units.index((t, half))
+            bank = banks[a_bank_of[u]]
             for a in range(PASSES):
                 head_pass(
                     bank, w1q[a][:, t * P : (t + 1) * P].bitcast(FP8X4), w1_sc[a][:, t * P : (t + 1) * P], a, half
@@ -204,57 +208,64 @@ def tile_list_crystal_disagreement_scores_kernel(
                 h_f32[:, :, lo:hi].rearrange("p t (c i) -> p c t i", i=4),
             )
 
+        o_bank_of = {0: 0, 256: 1, 512: 2, 768: 3, 896: 4}
         out_view = out.rearrange("(b p) j -> p b j", p=P)
 
-        def read_out(lo, hi):
+        def read_out(lo, hi, engine_copy, queue):
             nc.vector.quantize_mx(
                 out=hq[:, lo:hi].bitcast(FP8X4), scales=h_sc[:, lo:hi], in_=h_bf[:, lo * PACK : hi * PACK]
             )
-            for c0 in range(lo, hi, 256):
-                bank = psum.tile([P, 2, 256], F32, name="bank")
-                for b in range(N // P):
-                    nc.tensor.matmul_mx(
-                        out=bank[:, b, :],
-                        lhsT=w3q[:, b * P : (b + 1) * P].bitcast(FP8X4),
-                        lhsT_scale=w3_sc[:, b * P : (b + 1) * P],
-                        rhs=hq[:, c0 : c0 + 256].bitcast(FP8X4),
-                        rhs_scale=h_sc[:, c0 : c0 + 256],
-                        start=True,
-                        stop=True,
-                    )
-                res = ring.tile([P, 2, 256], F32, name="res")
-                nc.scalar.copy(res[:], bank[:])
-                nc.sync.dma_start(out_view[:, :, c0 : c0 + 256], res[:])
+            bank = banks[o_bank_of[lo]][:, 0 : (N // P) * (hi - lo)].rearrange("p (b j) -> p b j", b=N // P)
+            for b in range(N // P):
+                nc.tensor.matmul_mx(
+                    out=bank[:, b, :],
+                    lhsT=w3q[:, b * P : (b + 1) * P].bitcast(FP8X4),
+                    lhsT_scale=w3_sc[:, b * P : (b + 1) * P],
+                    rhs=hq[:, lo:hi].bitcast(FP8X4),
+                    rhs_scale=h_sc[:, lo:hi],
+                    start=True,
+                    stop=True,
+                )
+            res = keep.tile([P, N // P, hi - lo], F32, name=f"res{lo}")
+            engine_copy(res[:], bank[:])
+            queue.dma_start(out_view[:, :, lo:hi], res[:])
 
-        b_tanh(0)
-        b_tanh(1)
-        b_tanh(2)
+        for u in range(5):
+            b_tanh(u)
         squared_difference(*units[0])
-        for u in range(1, 5):
-            b_tanh(u + 2)
-            squared_difference(*units[u])
-            t, half = units[u - 1]
-            weigh(t, half * HALF, (half + 1) * HALF)
-        b_tanh(7)
-        squared_difference(*units[5])
-        weigh(3, 0, HALF)
-        squared_difference(*units[6])
-        squared_difference(*units[7])
+        squared_difference(*units[1])
         nc.scalar.copy(
             w3_bf[:].rearrange("p (c i j) -> p c j i", i=4, j=PACK),
             w3_raw[:].rearrange("p j (c i) -> p c j i", i=4),
         )
-        interleave_h(nc.scalar.copy, 0, 256)
-        interleave_h(nc.scalar.copy, 256, HALF)
-        weigh(1, HALF, S)
         nc.vector.quantize_mx(out=w3q[:].bitcast(FP8X4), scales=w3_sc[:], in_=w3_bf[:])
+        weigh(0, 0, HALF)
+        squared_difference(*units[2])
+        weigh(0, HALF, S)
+        squared_difference(*units[3])
+        b_tanh(5)
+        weigh(1, 0, HALF)
+        squared_difference(*units[4])
+        b_tanh(6)
+        weigh(2, 0, HALF)
+        squared_difference(*units[5])
+        b_tanh(7)
+        weigh(3, 0, HALF)
+        squared_difference(*units[6])
+        squared_difference(*units[7])
+        interleave_h(nc.scalar.copy, 0, 256)
+        read_out(0, 256, nc.scalar.copy, nc.sync)
+        interleave_h(nc.scalar.copy, 256, HALF)
+        read_out(256, HALF, nc.scalar.copy, nc.sync)
+        weigh(1, HALF, S)
         weigh(2, HALF, 768)
         weigh(3, HALF, 768)
         interleave_h(nc.scalar.copy, HALF, 768)
-        read_out(0, 256)
+        read_out(HALF, 768, nc.scalar.copy, nc.sync)
         weigh(2, 768, S)
-        read_out(256, HALF)
-        weigh(3, 768, S)
-        interleave_h(nc.vector.tensor_copy, 768, S)
-        read_out(HALF, 768)
-        read_out(768, S)
+        weigh(3, 768, 896)
+        weigh(3, 896, S)
+        interleave_h(nc.vector.tensor_copy, 768, 896)
+        interleave_h(nc.vector.tensor_copy, 896, S)
+        read_out(768, 896, nc.scalar.copy, nc.sync)
+        read_out(896, S, nc.vector.tensor_copy, nc.scalar)

@@ -29,7 +29,6 @@ def tile_list_crystal_disagreement_scores_kernel(
     nc = tc.nc
     with ExitStack() as ctx:
         keep = ctx.enter_context(tc.tile_pool(name="keep", bufs=1))
-        ring = ctx.enter_context(tc.tile_pool(name="ring", bufs=4))
         psum = ctx.enter_context(tc.psum_pool(name="psum", bufs=1))
 
         offsets = keep.tile([P, S // 16], U16, name="offsets")
@@ -50,7 +49,6 @@ def tile_list_crystal_disagreement_scores_kernel(
         w3q = keep.tile([P, N], U32, name="w3q", align_bytes=64)
         w3_sc = keep.tile([P, N], U8, name="w3_sc", align_bytes=64)
         tanh_b = keep.tile([P, PACK, S], F32, name="tanh_b")
-        sq = {}
         h_f32 = keep.tile([P, PACK, S], F32, name="h_f32")
         h_bf = keep.tile([P, S * PACK], BF16, name="h_bf", align_bytes=64)
         hq = keep.tile([P, S], U32, name="hq", align_bytes=64)
@@ -116,11 +114,10 @@ def tile_list_crystal_disagreement_scores_kernel(
         load_w1(2)
         g_rows = gT.rearrange("(p t) n -> p t n", t=PACK)
         w3_raw = keep.tile([P, PACK, N], F32, name="w3_raw")
+        nc.sync.dma_start(w3_raw[:], w3.rearrange("(p j) c -> p j c", j=PACK))
         for t in range(PACK):
             g_tab.setdefault(t, keep.tile([P, T], F32, name=f"g_tab{t}"))
             nc.sync.dma_start(g_tab[t][:], g_rows[:, t, :])
-            if t == 0:
-                nc.sync.dma_start(w3_raw[:], w3.rearrange("(p j) c -> p j c", j=PACK))
 
         nc.vector.tensor_copy(
             w2q[:].bitcast(U16).rearrange("p a (t m) -> p t a m", t=PACK),
@@ -131,12 +128,16 @@ def tile_list_crystal_disagreement_scores_kernel(
             w2_sc_raw[:].bitcast(U8).rearrange("p a (m t) -> p t a m", t=PACK),
         )
         gather_words(1, 0, S)
-        interleave_w1(nc.scalar.copy, 0, 0, PACK)
+        interleave_w1(nc.scalar.copy, 0, 0, 2)
+        interleave_w1(nc.scalar.copy, 0, 2, PACK)
         gather_words(2, 0, HALF)
         gather_words(2, HALF, S)
         quantize_w1(0, 0, PACK)
 
-        units = [(0, 0), (0, 1), (1, 0), (2, 0), (3, 0), (1, 1), (2, 1), (3, 1)]
+        units = [(t, half) for half in range(2) for t in range(PACK)]
+        tanh_a_ring = [keep.tile([P, HALF], F32, name=f"tanh_a{i}") for i in range(3)]
+        diff_ring = [keep.tile([P, HALF], F32, name=f"diff{i}") for i in range(4)]
+        sq_ring = [keep.tile([P, HALF], F32, name=f"sq{i}") for i in range(4)]
 
         def head_pass(bank, lhsT, lhsT_scale, a, half):
             cols = slice(half * HALF, (half + 1) * HALF)
@@ -150,8 +151,8 @@ def tile_list_crystal_disagreement_scores_kernel(
                 stop=(a == PASSES - 1),
             )
 
-        b_bank_of = [0,1,2,3,4,6,5,7]
-        a_bank_of = [5,6,7,5,7,6,5,6]
+        b_bank_of = [0, 1, 2, 3, 4, 7, 5, 6]
+        a_bank_of = [5, 6, 7, 5, 6, 7, 5, 6]
         banks = [psum.tile([P, HALF], F32, name=f"bank{i}") for i in range(8)]
         b_banks = [banks[i] for i in b_bank_of]
 
@@ -171,34 +172,33 @@ def tile_list_crystal_disagreement_scores_kernel(
                 b_pass(u, a)
             nc.scalar.activation(tanh_b[:, t, half * HALF : (half + 1) * HALF], b_banks[u][:], ACT.Tanh)
 
-        interleave_w1(nc.vector.tensor_copy, 1, 0, PACK)
-        quantize_w1(1, 0, PACK)
-        interleave_w1(nc.vector.tensor_copy, 2, 0, 2)
-        quantize_w1(2, 0, 2)
-        interleave_w1(nc.scalar.copy, 2, 2, PACK)
-        quantize_w1(2, 2, PACK)
 
-        def squared_difference(t, half):
-            cols = slice(half * HALF, (half + 1) * HALF)
-            u = units.index((t, half))
+        def a_tanh(u):
+            t, half = units[u]
             bank = banks[a_bank_of[u]]
             for a in range(PASSES):
                 head_pass(
                     bank, w1q[a][:, t * P : (t + 1) * P].bitcast(FP8X4), w1_sc[a][:, t * P : (t + 1) * P], a, half
                 )
-            tanh_a = ring.tile([P, HALF], F32, name="tanh_a")
-            nc.scalar.activation(tanh_a[:], bank[:], ACT.Tanh)
-            diff = ring.tile([P, HALF], F32, name="diff", bufs=2)
-            nc.vector.tensor_tensor(diff[:], tanh_a[:], tanh_b[:, t, cols], ALU.subtract)
-            sq.setdefault((t, half), ring.tile([P, HALF], F32, name="sq", bufs=3))
-            nc.scalar.activation(sq[t, half][:], diff[:], ACT.Square)
+            nc.scalar.activation(tanh_a_ring[u % len(tanh_a_ring)][:], bank[:], ACT.Tanh)
+
+        def squared_difference(u):
+            t, half = units[u]
+            diff = diff_ring[u % len(diff_ring)]
+            nc.vector.tensor_tensor(
+                diff[:],
+                tanh_a_ring[u % len(tanh_a_ring)][:],
+                tanh_b[:, t, half * HALF : (half + 1) * HALF],
+                ALU.subtract,
+            )
+            nc.scalar.activation(sq_ring[u % len(sq_ring)][:], diff[:], ACT.Square)
 
         def weigh(t, lo, hi):
             half, start = divmod(lo, HALF)
             nc.vector.tensor_tensor(
                 h_f32[:, t, lo:hi],
                 g_tab[t][:].indirect(listed(lo, hi)),
-                sq[t, half][:, start : start + hi - lo],
+                sq_ring[units.index((t, half)) % len(sq_ring)][:, start : start + hi - lo],
                 ALU.mult,
             )
 
@@ -230,42 +230,60 @@ def tile_list_crystal_disagreement_scores_kernel(
             engine_copy(res[:], bank[:])
             queue.dma_start(out_view[:, :, lo:hi], res[:])
 
-        for u in range(5):
-            b_tanh(u)
-        squared_difference(*units[0])
-        squared_difference(*units[1])
+        interleave_w1(nc.vector.tensor_copy, 1, 0, 2)
+        interleave_w1(nc.vector.tensor_copy, 1, 2, 4)
+        quantize_w1(1, 0, PACK)
+        interleave_w1(nc.vector.tensor_copy, 2, 0, 2)
+        quantize_w1(2, 0, 2)
+        interleave_w1(nc.scalar.copy, 2, 2, PACK)
+        quantize_w1(2, 2, PACK)
+        b_tanh(0)
+        b_tanh(1)
+        b_tanh(2)
+        b_tanh(3)
+        b_tanh(4)
         nc.scalar.copy(
             w3_bf[:].rearrange("p (c i j) -> p c j i", i=4, j=PACK),
             w3_raw[:].rearrange("p j (c i) -> p c j i", i=4),
         )
         nc.vector.quantize_mx(out=w3q[:].bitcast(FP8X4), scales=w3_sc[:], in_=w3_bf[:])
-        weigh(0, 0, HALF)
-        squared_difference(*units[2])
-        weigh(0, HALF, S)
-        squared_difference(*units[3])
+        a_tanh(0)
+        a_tanh(1)
+        a_tanh(2)
+        squared_difference(0)
+        squared_difference(1)
+        squared_difference(2)
+        a_tanh(3)
+        weigh(0, 0, 512)
+        a_tanh(4)
+        weigh(1, 0, 512)
+        squared_difference(3)
         b_tanh(5)
-        weigh(1, 0, HALF)
-        squared_difference(*units[4])
+        a_tanh(5)
+        squared_difference(4)
+        weigh(2, 0, 512)
         b_tanh(6)
-        weigh(2, 0, HALF)
-        squared_difference(*units[5])
+        a_tanh(6)
+        weigh(3, 0, 512)
+        squared_difference(5)
         b_tanh(7)
-        weigh(3, 0, HALF)
-        squared_difference(*units[6])
-        squared_difference(*units[7])
+        a_tanh(7)
         interleave_h(nc.scalar.copy, 0, 256)
+        weigh(0, 512, 1024)
+        squared_difference(6)
+        interleave_h(nc.scalar.copy, 256, 512)
+        squared_difference(7)
         read_out(0, 256, nc.scalar.copy, nc.sync)
-        interleave_h(nc.scalar.copy, 256, HALF)
-        read_out(256, HALF, nc.scalar.copy, nc.sync)
-        weigh(1, HALF, S)
-        weigh(2, HALF, 768)
-        weigh(3, HALF, 768)
-        interleave_h(nc.scalar.copy, HALF, 768)
-        read_out(HALF, 768, nc.scalar.copy, nc.sync)
-        weigh(2, 768, S)
+        weigh(1, 512, 1024)
+        read_out(256, 512, nc.scalar.copy, nc.sync)
+        weigh(2, 512, 768)
+        weigh(3, 512, 768)
+        interleave_h(nc.scalar.copy, 512, 768)
+        weigh(2, 768, 1024)
         weigh(3, 768, 896)
-        weigh(3, 896, S)
+        weigh(3, 896, 1024)
         interleave_h(nc.vector.tensor_copy, 768, 896)
-        interleave_h(nc.vector.tensor_copy, 896, S)
-        read_out(768, 896, nc.scalar.copy, nc.sync)
-        read_out(896, S, nc.vector.tensor_copy, nc.scalar)
+        interleave_h(nc.vector.tensor_copy, 896, 1024)
+        read_out(512, 768, nc.scalar.copy, nc.sync)
+        read_out(768, 896, nc.vector.tensor_copy, nc.sync)
+        read_out(896, 1024, nc.scalar.copy, nc.scalar)

@@ -1,6 +1,7 @@
 from contextlib import ExitStack
 
 import concourse.mybir as mybir
+from concourse.masks import make_identity
 
 K, T, S, H, N = 1536, 2048, 1024, 512, 256
 FLOPS = 2 * (2 * K * H * S + H * N * S)
@@ -20,6 +21,7 @@ P = 128
 PACK = 4
 PASSES = K // (P * PACK)
 HALF = S // 2
+RUN = 8
 MOVED_ROWS = 112
 
 
@@ -32,7 +34,10 @@ def tile_list_crystal_disagreement_scores_kernel(
         psum = ctx.enter_context(tc.psum_pool(name="psum", bufs=1))
 
         offsets = keep.tile([P, S // 16], U16, name="offsets")
-        tab, w1_raw, g_tab = {}, {}, {}
+        tab = [keep.tile([P, T], I32, name=f"tab{a}") for a in range(PASSES)]
+        w1_raw = [keep.tile([P, PACK, H], F32, name=f"w1_raw{a}") for a in range(PASSES)]
+        g_tab = [keep.tile([P, T], F32, name=f"g_tab{t}") for t in range(PACK)]
+        w3_raw = keep.tile([P, PACK, N], F32, name="w3_raw")
         tab_sc = keep.tile([P, T // 4], I32, name="tab_sc")
         w2_raw = keep.tile([P, PASSES, H // 2], I32, name="w2_raw")
         w2_sc_raw = keep.tile([P, PASSES, H // 4], I32, name="w2_sc_raw")
@@ -40,16 +45,15 @@ def tile_list_crystal_disagreement_scores_kernel(
         v = [keep.tile([P, S], U32, name=f"v{a}", align_bytes=64) for a in range(PASSES)]
         v_sc0 = keep.tile([P, S], U8, name="v_sc0", align_bytes=64)
         v_sc_moved = [keep.tile([P, S // 4], I32, name=f"v_sc_moved{a}", align_bytes=64) for a in range(1, PASSES)]
-        w2q = keep.tile([P, PASSES, 2 * H], U8, name="w2q", align_bytes=64)
-        w2_sc = keep.tile([P, PASSES, H], U8, name="w2_sc", align_bytes=64)
+        w2q = keep.tile([P, PASSES, H // 2], I32, name="w2q", align_bytes=64)
+        w2_sc = keep.tile([P, PASSES, H // 4], I32, name="w2_sc", align_bytes=64)
         w1_bf = [keep.tile([P, PACK * H], BF16, name=f"w1_bf{a}", align_bytes=64) for a in range(PASSES)]
         w1q = [keep.tile([P, H], U32, name=f"w1q{a}", align_bytes=64) for a in range(PASSES)]
         w1_sc = [keep.tile([P, H], U8, name=f"w1_sc{a}", align_bytes=64) for a in range(PASSES)]
         w3_bf = keep.tile([P, PACK * N], BF16, name="w3_bf", align_bytes=64)
-        w3q = keep.tile([P, N], U32, name="w3q", align_bytes=64)
         w3_sc = keep.tile([P, N], U8, name="w3_sc", align_bytes=64)
-        tanh_b = keep.tile([P, PACK, S], F32, name="tanh_b")
-        h_f32 = keep.tile([P, PACK, S], F32, name="h_f32")
+        h_slots = [keep.tile([P, PACK, 256], F32, name=f"h_slot{i}") for i in range(3)]
+        h_slot_of = {0: 0, 256: 1, 512: 2, 768: 0, 896: 1}
         h_bf = keep.tile([P, S * PACK], BF16, name="h_bf", align_bytes=64)
         hq = keep.tile([P, S], U32, name="hq", align_bytes=64)
         h_sc = keep.tile([P, S], U8, name="h_sc", align_bytes=64)
@@ -58,21 +62,22 @@ def tile_list_crystal_disagreement_scores_kernel(
             return offsets[:, lo // 16 : hi // 16]
 
         def load_tab(a):
-            tab.setdefault(a, keep.tile([P, T], I32, name=f"tab{a}"))
             nc.sync.dma_start(tab[a][:], tab_words[a].rearrange("p n i -> p (n i)").bitcast(I32))
 
+        def load_tab_scales(queue, q):
+            queue.dma_start(tab_sc[32 * q : 32 * q + 4 * PASSES, :], tab_scales[:, 4 * q : 4 * q + 4, :].bitcast(I32))
+
         def load_w1(a):
-            w1_raw.setdefault(a, keep.tile([P, PACK, H], F32, name=f"w1_raw{a}"))
             rows = w1[a * P * PACK : (a + 1) * P * PACK, :]
             nc.sync.dma_start(w1_raw[a][:], rows.rearrange("(p j) c -> p j c", j=PACK))
 
         def gather_words(a, lo, hi):
             nc.vector.tensor_copy(v[a][:, lo:hi], tab[a][:].bitcast(U32).indirect(listed(lo, hi)))
 
-        def interleave_w1(engine_copy, a, t0, t1):
+        def interleave_w1(engine_copy, a, t):
             engine_copy(
-                w1_bf[a][:].rearrange("p (t m j) -> p m j t", t=PACK, j=PACK)[:, :, :, t0:t1],
-                w1_raw[a][:].rearrange("p j (m t) -> p m j t", t=PACK)[:, :, :, t0:t1],
+                w1_bf[a][:, t * H : (t + 1) * H].rearrange("p (q h l j) -> p q h j l", h=2, l=4, j=PACK),
+                w1_raw[a][:].rearrange("p j (q t h l) -> p t q h j l", t=PACK, h=2, l=4)[:, t],
             )
 
         def quantize_w1(a, t0, t1):
@@ -84,14 +89,17 @@ def tile_list_crystal_disagreement_scores_kernel(
 
         nc.gpsimd.memset(tab_sc[:], 0)
         nc.gpsimd.memset(w2_sc_raw[:], 0)
+        ident = keep.tile([P, P], F32, name="ident")
+        make_identity(nc, ident[:])
         for moved in v_sc_moved:
             nc.vector.memset(moved[:], 0)
         nc.sync.dma_start(offsets[:], offs)
         load_tab(0)
-        for q in range(4):
-            nc.sync.dma_start(
-                tab_sc[32 * q : 32 * q + 4 * PASSES, :], tab_scales[:, 4 * q : 4 * q + 4, :].bitcast(I32)
-            )
+        load_tab_scales(nc.scalar, 2)
+        load_tab_scales(nc.scalar, 3)
+        load_tab_scales(nc.sync, 0)
+        load_tab_scales(nc.sync, 1)
+        load_w1(0)
         nc.sync.dma_start(w2_raw[:], w2_words.rearrange("a p c -> p a c").bitcast(I32))
         for q in range(4):
             nc.sync.dma_start(
@@ -100,122 +108,131 @@ def tile_list_crystal_disagreement_scores_kernel(
             )
         load_tab(1)
         load_tab(2)
-        load_w1(0)
 
         gather_words(0, 0, S)
         nc.vector.tensor_copy(v_sc0[:], tab_sc[:].bitcast(U8).indirect(offsets[:]))
         for a in range(1, PASSES):
-            nc.sync.dma_start(
-                v_sc_moved[a - 1][0:MOVED_ROWS, :], v_sc0[4 * a : 4 * a + MOVED_ROWS, :].bitcast(I32)
-            )
+            nc.sync.dma_start(v_sc_moved[a - 1][0:MOVED_ROWS, :], v_sc0[4 * a : 4 * a + MOVED_ROWS, :].bitcast(I32))
         v_sc = [v_sc0[:]] + [moved[:].bitcast(U8) for moved in v_sc_moved]
 
         load_w1(1)
         load_w1(2)
-        g_rows = gT.rearrange("(p t) n -> p t n", t=PACK)
-        w3_raw = keep.tile([P, PACK, N], F32, name="w3_raw")
-        nc.sync.dma_start(w3_raw[:], w3.rearrange("(p j) c -> p j c", j=PACK))
+        g_rows = gT.rearrange("(q t i) n -> t q i n", t=PACK, i=RUN)
+        w3_rows = w3.rearrange("(q t i) n -> t q i n", t=PACK, i=RUN)
+        for t in range(PACK - 1):
+            nc.sync.dma_start(g_tab[t][:], g_rows[t])
         for t in range(PACK):
-            g_tab.setdefault(t, keep.tile([P, T], F32, name=f"g_tab{t}"))
-            nc.sync.dma_start(g_tab[t][:], g_rows[:, t, :])
+            nc.sync.dma_start(w3_raw[:, t, :], w3_rows[t])
+        nc.sync.dma_start(g_tab[PACK - 1][:], g_rows[PACK - 1])
 
+        for t in range(PACK):
+            interleave_w1(nc.scalar.copy, 0, t)
+        quantize_w1(0, 0, PACK)
         nc.vector.tensor_copy(
-            w2q[:].bitcast(U16).rearrange("p a (t m) -> p t a m", t=PACK),
-            w2_raw[:].bitcast(U16).rearrange("p a (m t) -> p t a m", t=PACK),
+            w2q[:].rearrange("p a (t q w) -> p t a q w", t=PACK, w=4),
+            w2_raw[:].rearrange("p a (q t w) -> p t a q w", t=PACK, w=4),
         )
         nc.vector.tensor_copy(
-            w2_sc[:].rearrange("p a (t m) -> p t a m", t=PACK),
-            w2_sc_raw[:].bitcast(U8).rearrange("p a (m t) -> p t a m", t=PACK),
+            w2_sc[:].rearrange("p a (t q w) -> p t a q w", t=PACK, w=2),
+            w2_sc_raw[:].rearrange("p a (q t w) -> p t a q w", t=PACK, w=2),
         )
-        gather_words(1, 0, S)
-        interleave_w1(nc.scalar.copy, 0, 0, 2)
-        interleave_w1(nc.scalar.copy, 0, 2, PACK)
+        gather_words(1, 0, HALF)
+        gather_words(1, HALF, S)
         gather_words(2, 0, HALF)
         gather_words(2, HALF, S)
-        quantize_w1(0, 0, PACK)
+        for t in range(PACK):
+            interleave_w1(nc.vector.tensor_copy, 1, t)
+        quantize_w1(1, 0, PACK)
+        interleave_w1(nc.vector.tensor_copy, 2, 0)
+        interleave_w1(nc.vector.tensor_copy, 2, 1)
+        quantize_w1(2, 0, 1)
+        interleave_w1(nc.vector.tensor_copy, 2, 2)
+        quantize_w1(2, 1, 2)
+        interleave_w1(nc.vector.tensor_copy, 2, 3)
+        quantize_w1(2, 2, 4)
 
-        units = [(t, half) for half in range(2) for t in range(PACK)]
-        tanh_a_ring = [keep.tile([P, HALF], F32, name=f"tanh_a{i}") for i in range(3)]
-        diff_ring = [keep.tile([P, HALF], F32, name=f"diff{i}") for i in range(4)]
-        sq_ring = [keep.tile([P, HALF], F32, name=f"sq{i}") for i in range(4)]
-
-        def head_pass(bank, lhsT, lhsT_scale, a, half):
-            cols = slice(half * HALF, (half + 1) * HALF)
-            nc.tensor.matmul_mx(
-                out=bank[:],
-                lhsT=lhsT,
-                lhsT_scale=lhsT_scale,
-                rhs=v[a][:, cols].bitcast(FP8X4),
-                rhs_scale=v_sc[a][:, cols],
-                start=(a == 0),
-                stop=(a == PASSES - 1),
-            )
-
-        b_bank_of = [0, 1, 2, 3, 4, 7, 5, 6]
-        a_bank_of = [5, 6, 7, 5, 6, 7, 5, 6]
+        tanh_a = [keep.tile([P, HALF], F32, name=f"tanh_a{u}") for u in range(8)]
+        tanh_b = [keep.tile([P, HALF], F32, name=f"tanh_b{u}") for u in range(8)]
+        sq_first = [keep.tile([P, HALF], F32, name=f"sq{t}", align_bytes=64) for t in range(PACK)]
+        sq_second = keep.tile([P, PACK, HALF], F32, name="sq_second")
+        w3q = keep.tile([P, N], U32, name="w3q", align_bytes=64)
         banks = [psum.tile([P, HALF], F32, name=f"bank{i}") for i in range(8)]
-        b_banks = [banks[i] for i in b_bank_of]
 
-        def b_pass(u, a):
-            t, half = units[u]
-            head_pass(
-                b_banks[u],
-                w2q[:, a, 2 * t * P : 2 * (t + 1) * P].bitcast(FP4X4),
-                w2_sc[:, a, t * P : (t + 1) * P],
-                a,
-                half,
-            )
-
-        def b_tanh(u):
-            t, half = units[u]
+        def passes(bank, stationary, moving):
             for a in range(PASSES):
-                b_pass(u, a)
-            nc.scalar.activation(tanh_b[:, t, half * HALF : (half + 1) * HALF], b_banks[u][:], ACT.Tanh)
-
-
-        def a_tanh(u):
-            t, half = units[u]
-            bank = banks[a_bank_of[u]]
-            for a in range(PASSES):
-                head_pass(
-                    bank, w1q[a][:, t * P : (t + 1) * P].bitcast(FP8X4), w1_sc[a][:, t * P : (t + 1) * P], a, half
+                nc.tensor.matmul_mx(
+                    out=bank[:],
+                    lhsT=stationary(a)[0],
+                    lhsT_scale=stationary(a)[1],
+                    rhs=moving(a)[0],
+                    rhs_scale=moving(a)[1],
+                    start=(a == 0),
+                    stop=(a == PASSES - 1),
                 )
-            nc.scalar.activation(tanh_a_ring[u % len(tanh_a_ring)][:], bank[:], ACT.Tanh)
 
-        def squared_difference(u):
-            t, half = units[u]
-            diff = diff_ring[u % len(diff_ring)]
-            nc.vector.tensor_tensor(
-                diff[:],
-                tanh_a_ring[u % len(tanh_a_ring)][:],
-                tanh_b[:, t, half * HALF : (half + 1) * HALF],
-                ALU.subtract,
+        def tokens(lo, hi):
+            return lambda a: (v[a][:, lo:hi].bitcast(FP8X4), v_sc[a][:, lo:hi])
+
+        def w1_cols(lo, hi):
+            return lambda a: (w1q[a][:, lo:hi].bitcast(FP8X4), w1_sc[a][:, lo:hi])
+
+        def w2_cols(lo, hi):
+            return lambda a: (
+                w2q[:, a, :].bitcast(U8)[:, 2 * lo : 2 * hi].bitcast(FP4X4),
+                w2_sc[:, a, :].bitcast(U8)[:, lo:hi],
             )
-            nc.scalar.activation(sq_ring[u % len(sq_ring)][:], diff[:], ACT.Square)
+
+        def head_b(t):
+            passes(banks[t], w2_cols(t * P, (t + 1) * P), tokens(0, HALF))
+            nc.scalar.activation(tanh_b[t][:], banks[t][:], ACT.Tanh)
+
+        def head_a(t):
+            passes(banks[4 + t], w1_cols(t * P, (t + 1) * P), tokens(0, HALF))
+            nc.scalar.activation(tanh_a[t][:], banks[4 + t][:], ACT.Tanh)
+
+        def squared_difference(t):
+            nc.vector.tensor_tensor(sq_first[t][:], tanh_a[t][:], tanh_b[t][:], ALU.subtract)
+            nc.scalar.activation(sq_first[t][:], sq_first[t][:], ACT.Square)
+
+        def block_b(j):
+            bank = banks[(0, 1, 4, 5)[j]]
+            passes(bank, tokens(HALF + j * P, HALF + (j + 1) * P), w2_cols(0, H))
+            nc.scalar.activation(tanh_b[4 + j][:], bank[:], ACT.Tanh, scale=-1.0)
+
+        def block_a(j):
+            bank = banks[(6, 7, 4, 5)[j]]
+            passes(bank, tokens(HALF + j * P, HALF + (j + 1) * P), w1_cols(0, H))
+            nc.scalar.activation(tanh_a[4 + j][:], bank[:], ACT.Tanh)
+
+        def block_square(j):
+            bank = banks[(2, 3, 0, 1)[j]]
+            for t in range(PACK):
+                cols = slice(t * P, (t + 1) * P)
+                nc.tensor.matmul(bank[:, cols], tanh_a[4 + j][:, cols], ident[:], start=True, stop=False, is_transpose=True)
+                nc.tensor.matmul(bank[:, cols], tanh_b[4 + j][:, cols], ident[:], start=False, stop=True, is_transpose=True)
+            nc.scalar.activation(
+                sq_second[:, :, j * P : (j + 1) * P], bank[:].rearrange("p (t c) -> p t c", t=PACK), ACT.Square
+            )
 
         def weigh(t, lo, hi):
-            half, start = divmod(lo, HALF)
+            sq = sq_first[t][:, lo:hi] if lo < HALF else sq_second[:, t, lo - HALF : hi - HALF]
             nc.vector.tensor_tensor(
-                h_f32[:, t, lo:hi],
-                g_tab[t][:].indirect(listed(lo, hi)),
-                sq_ring[units.index((t, half)) % len(sq_ring)][:, start : start + hi - lo],
-                ALU.mult,
+                h_slots[h_slot_of[lo]][:, t, 0 : hi - lo], g_tab[t][:].indirect(listed(lo, hi)), sq, ALU.mult
             )
 
         def interleave_h(engine_copy, lo, hi):
             engine_copy(
                 h_bf[:, lo * PACK : hi * PACK].rearrange("p (c i t) -> p c t i", i=4, t=PACK),
-                h_f32[:, :, lo:hi].rearrange("p t (c i) -> p c t i", i=4),
+                h_slots[h_slot_of[lo]][:, :, 0 : hi - lo].rearrange("p t (c i) -> p c t i", i=4),
             )
 
-        o_bank_of = {0: 0, 256: 1, 512: 2, 768: 3, 896: 4}
         out_view = out.rearrange("(b p) j -> p b j", p=P)
 
-        def read_out(lo, hi, engine_copy, queue):
+        def read_out(o, lo, hi, engine_copy, queue):
             nc.vector.quantize_mx(
                 out=hq[:, lo:hi].bitcast(FP8X4), scales=h_sc[:, lo:hi], in_=h_bf[:, lo * PACK : hi * PACK]
             )
-            bank = banks[o_bank_of[lo]][:, 0 : (N // P) * (hi - lo)].rearrange("p (b j) -> p b j", b=N // P)
+            bank = banks[o][:, 0 : (N // P) * (hi - lo)].rearrange("p (b j) -> p b j", b=N // P)
             for b in range(N // P):
                 nc.tensor.matmul_mx(
                     out=bank[:, b, :],
@@ -230,60 +247,50 @@ def tile_list_crystal_disagreement_scores_kernel(
             engine_copy(res[:], bank[:])
             queue.dma_start(out_view[:, :, lo:hi], res[:])
 
-        interleave_w1(nc.vector.tensor_copy, 1, 0, 2)
-        interleave_w1(nc.vector.tensor_copy, 1, 2, 4)
-        quantize_w1(1, 0, PACK)
-        interleave_w1(nc.vector.tensor_copy, 2, 0, 2)
-        quantize_w1(2, 0, 2)
-        interleave_w1(nc.scalar.copy, 2, 2, PACK)
-        quantize_w1(2, 2, PACK)
-        b_tanh(0)
-        b_tanh(1)
-        b_tanh(2)
-        b_tanh(3)
-        b_tanh(4)
-        nc.scalar.copy(
+        def weigh_first_half(t):
+            weigh(t, 0, 256)
+            weigh(t, 256, 512)
+
+        for t in range(PACK):
+            head_b(t)
+        block_b(0)
+        block_b(1)
+        for t in range(PACK):
+            head_a(t)
+        for t in range(PACK):
+            squared_difference(t)
+        weigh_first_half(0)
+        weigh_first_half(1)
+        weigh_first_half(2)
+        block_a(0)
+        block_a(1)
+        block_square(0)
+        block_square(1)
+        block_b(2)
+        block_a(2)
+        block_square(2)
+        nc.vector.tensor_copy(
             w3_bf[:].rearrange("p (c i j) -> p c j i", i=4, j=PACK),
             w3_raw[:].rearrange("p j (c i) -> p c j i", i=4),
         )
+        weigh_first_half(3)
         nc.vector.quantize_mx(out=w3q[:].bitcast(FP8X4), scales=w3_sc[:], in_=w3_bf[:])
-        a_tanh(0)
-        a_tanh(1)
-        a_tanh(2)
-        squared_difference(0)
-        squared_difference(1)
-        squared_difference(2)
-        a_tanh(3)
-        weigh(0, 0, 512)
-        a_tanh(4)
-        weigh(1, 0, 512)
-        squared_difference(3)
-        b_tanh(5)
-        a_tanh(5)
-        squared_difference(4)
-        weigh(2, 0, 512)
-        b_tanh(6)
-        a_tanh(6)
-        weigh(3, 0, 512)
-        squared_difference(5)
-        b_tanh(7)
-        a_tanh(7)
         interleave_h(nc.scalar.copy, 0, 256)
-        weigh(0, 512, 1024)
-        squared_difference(6)
+        block_b(3)
+        block_a(3)
+        block_square(3)
         interleave_h(nc.scalar.copy, 256, 512)
-        squared_difference(7)
-        read_out(0, 256, nc.scalar.copy, nc.sync)
-        weigh(1, 512, 1024)
-        read_out(256, 512, nc.scalar.copy, nc.sync)
-        weigh(2, 512, 768)
-        weigh(3, 512, 768)
+        for t in range(PACK):
+            weigh(t, 512, 768)
+        read_out(6, 0, 256, nc.scalar.copy, nc.sync)
         interleave_h(nc.scalar.copy, 512, 768)
-        weigh(2, 768, 1024)
-        weigh(3, 768, 896)
-        weigh(3, 896, 1024)
-        interleave_h(nc.vector.tensor_copy, 768, 896)
+        for t in range(PACK):
+            weigh(t, 768, 896)
+        read_out(7, 256, 512, nc.scalar.copy, nc.sync)
+        interleave_h(nc.scalar.copy, 768, 896)
+        for t in range(PACK):
+            weigh(t, 896, 1024)
+        read_out(2, 512, 768, nc.scalar.copy, nc.sync)
         interleave_h(nc.vector.tensor_copy, 896, 1024)
-        read_out(512, 768, nc.scalar.copy, nc.sync)
-        read_out(768, 896, nc.vector.tensor_copy, nc.sync)
-        read_out(896, 1024, nc.scalar.copy, nc.scalar)
+        read_out(3, 768, 896, nc.scalar.copy, nc.sync)
+        read_out(4, 896, 1024, nc.vector.tensor_copy, nc.scalar)

@@ -21,7 +21,6 @@ P = 128
 PACK = 4
 PASSES = K // (P * PACK)
 HALF = S // 2
-RUN = 8
 MOVED_ROWS = 112
 
 
@@ -53,7 +52,7 @@ def tile_list_crystal_disagreement_scores_kernel(
         w3_bf = keep.tile([P, PACK * N], BF16, name="w3_bf", align_bytes=64)
         w3_sc = keep.tile([P, N], U8, name="w3_sc", align_bytes=64)
         h_slots = [keep.tile([P, PACK, 256], F32, name=f"h_slot{i}") for i in range(3)]
-        h_slot_of = {0: 0, 256: 1, 512: 2, 768: 0, 896: 1}
+        h_slot_of = {0: 0, 256: 1, 512: 2, 768: 0, 896: 2}
         h_bf = keep.tile([P, S * PACK], BF16, name="h_bf", align_bytes=64)
         hq = keep.tile([P, S], U32, name="hq", align_bytes=64)
         h_sc = keep.tile([P, S], U8, name="h_sc", align_bytes=64)
@@ -74,10 +73,10 @@ def tile_list_crystal_disagreement_scores_kernel(
         def gather_words(a, lo, hi):
             nc.vector.tensor_copy(v[a][:, lo:hi], tab[a][:].bitcast(U32).indirect(listed(lo, hi)))
 
-        def interleave_w1(engine_copy, a, t):
+        def interleave_w1(engine_copy, a, t0, t1):
             engine_copy(
-                w1_bf[a][:, t * H : (t + 1) * H].rearrange("p (q h l j) -> p q h j l", h=2, l=4, j=PACK),
-                w1_raw[a][:].rearrange("p j (q t h l) -> p t q h j l", t=PACK, h=2, l=4)[:, t],
+                w1_bf[a][:].rearrange("p (t m j) -> p m j t", t=PACK, j=PACK)[:, :, :, t0:t1],
+                w1_raw[a][:].rearrange("p j (m t) -> p m j t", t=PACK)[:, :, :, t0:t1],
             )
 
         def quantize_w1(a, t0, t1):
@@ -117,43 +116,36 @@ def tile_list_crystal_disagreement_scores_kernel(
 
         load_w1(1)
         load_w1(2)
-        g_rows = gT.rearrange("(q t i) n -> t q i n", t=PACK, i=RUN)
-        w3_rows = w3.rearrange("(q t i) n -> t q i n", t=PACK, i=RUN)
-        for t in range(PACK - 1):
-            nc.sync.dma_start(g_tab[t][:], g_rows[t])
+        g_rows = gT.rearrange("(p t) n -> p t n", t=PACK)
+        nc.sync.dma_start(w3_raw[:], w3.rearrange("(p j) c -> p j c", j=PACK))
         for t in range(PACK):
-            nc.sync.dma_start(w3_raw[:, t, :], w3_rows[t])
-        nc.sync.dma_start(g_tab[PACK - 1][:], g_rows[PACK - 1])
+            nc.sync.dma_start(g_tab[t][:], g_rows[:, t, :])
 
-        for t in range(PACK):
-            interleave_w1(nc.scalar.copy, 0, t)
+        nc.vector.tensor_copy(
+            w2q[:].bitcast(U16).rearrange("p a (t m) -> p t a m", t=PACK),
+            w2_raw[:].bitcast(U16).rearrange("p a (m t) -> p t a m", t=PACK),
+        )
+        nc.vector.tensor_copy(
+            w2_sc[:].bitcast(U8).rearrange("p a (t m) -> p t a m", t=PACK),
+            w2_sc_raw[:].bitcast(U8).rearrange("p a (m t) -> p t a m", t=PACK),
+        )
+        interleave_w1(nc.scalar.copy, 0, 0, 2)
+        interleave_w1(nc.scalar.copy, 0, 2, 4)
         quantize_w1(0, 0, PACK)
-        nc.vector.tensor_copy(
-            w2q[:].rearrange("p a (t q w) -> p t a q w", t=PACK, w=4),
-            w2_raw[:].rearrange("p a (q t w) -> p t a q w", t=PACK, w=4),
-        )
-        nc.vector.tensor_copy(
-            w2_sc[:].rearrange("p a (t q w) -> p t a q w", t=PACK, w=2),
-            w2_sc_raw[:].rearrange("p a (q t w) -> p t a q w", t=PACK, w=2),
-        )
         gather_words(1, 0, HALF)
         gather_words(1, HALF, S)
         gather_words(2, 0, HALF)
         gather_words(2, HALF, S)
-        for t in range(PACK):
-            interleave_w1(nc.vector.tensor_copy, 1, t)
-        quantize_w1(1, 0, PACK)
-        interleave_w1(nc.vector.tensor_copy, 2, 0)
-        interleave_w1(nc.vector.tensor_copy, 2, 1)
-        quantize_w1(2, 0, 1)
-        interleave_w1(nc.vector.tensor_copy, 2, 2)
-        quantize_w1(2, 1, 2)
-        interleave_w1(nc.vector.tensor_copy, 2, 3)
-        quantize_w1(2, 2, 4)
+        for a in range(1, PASSES):
+            interleave_w1(nc.vector.tensor_copy, a, 0, 2)
+            interleave_w1(nc.vector.tensor_copy, a, 2, 4)
+            quantize_w1(a, 0, 2)
+            quantize_w1(a, 2, 4)
 
         tanh_a = [keep.tile([P, HALF], F32, name=f"tanh_a{u}") for u in range(8)]
         tanh_b = [keep.tile([P, HALF], F32, name=f"tanh_b{u}") for u in range(8)]
-        sq_first = [keep.tile([P, HALF], F32, name=f"sq{t}", align_bytes=64) for t in range(PACK)]
+        sq_first = [keep.tile([P, HALF], F32, name=f"sq{t}")[:] for t in range(PACK - 1)]
+        sq_first.append(h_slots[2][:].rearrange("p t c -> p (t c)")[:, P : P + HALF])
         sq_second = keep.tile([P, PACK, HALF], F32, name="sq_second")
         w3q = keep.tile([P, N], U32, name="w3q", align_bytes=64)
         banks = [psum.tile([P, HALF], F32, name=f"bank{i}") for i in range(8)]
@@ -191,8 +183,8 @@ def tile_list_crystal_disagreement_scores_kernel(
             nc.scalar.activation(tanh_a[t][:], banks[4 + t][:], ACT.Tanh)
 
         def squared_difference(t):
-            nc.vector.tensor_tensor(sq_first[t][:], tanh_a[t][:], tanh_b[t][:], ALU.subtract)
-            nc.scalar.activation(sq_first[t][:], sq_first[t][:], ACT.Square)
+            nc.vector.tensor_tensor(sq_first[t], tanh_a[t][:], tanh_b[t][:], ALU.subtract)
+            nc.scalar.activation(sq_first[t], sq_first[t], ACT.Square)
 
         def block_b(j):
             bank = banks[(0, 1, 4, 5)[j]]
@@ -200,7 +192,7 @@ def tile_list_crystal_disagreement_scores_kernel(
             nc.scalar.activation(tanh_b[4 + j][:], bank[:], ACT.Tanh, scale=-1.0)
 
         def block_a(j):
-            bank = banks[(6, 7, 4, 5)[j]]
+            bank = banks[(6, 7, 6, 7)[j]]
             passes(bank, tokens(HALF + j * P, HALF + (j + 1) * P), w1_cols(0, H))
             nc.scalar.activation(tanh_a[4 + j][:], bank[:], ACT.Tanh)
 
@@ -264,10 +256,12 @@ def tile_list_crystal_disagreement_scores_kernel(
         weigh_first_half(2)
         block_a(0)
         block_a(1)
-        block_square(0)
-        block_square(1)
         block_b(2)
         block_a(2)
+        block_square(0)
+        block_square(1)
+        block_b(3)
+        block_a(3)
         block_square(2)
         nc.vector.tensor_copy(
             w3_bf[:].rearrange("p (c i j) -> p c j i", i=4, j=PACK),
@@ -276,21 +270,19 @@ def tile_list_crystal_disagreement_scores_kernel(
         weigh_first_half(3)
         nc.vector.quantize_mx(out=w3q[:].bitcast(FP8X4), scales=w3_sc[:], in_=w3_bf[:])
         interleave_h(nc.scalar.copy, 0, 256)
-        block_b(3)
-        block_a(3)
         block_square(3)
         interleave_h(nc.scalar.copy, 256, 512)
         for t in range(PACK):
             weigh(t, 512, 768)
-        read_out(6, 0, 256, nc.scalar.copy, nc.sync)
         interleave_h(nc.scalar.copy, 512, 768)
+        read_out(4, 0, 256, nc.scalar.copy, nc.sync)
         for t in range(PACK):
             weigh(t, 768, 896)
-        read_out(7, 256, 512, nc.scalar.copy, nc.sync)
         interleave_h(nc.scalar.copy, 768, 896)
+        read_out(5, 256, 512, nc.scalar.copy, nc.sync)
+        read_out(2, 512, 768, nc.scalar.copy, nc.sync)
         for t in range(PACK):
             weigh(t, 896, 1024)
-        read_out(2, 512, 768, nc.scalar.copy, nc.sync)
         interleave_h(nc.vector.tensor_copy, 896, 1024)
         read_out(3, 768, 896, nc.scalar.copy, nc.sync)
         read_out(4, 896, 1024, nc.vector.tensor_copy, nc.scalar)

@@ -51,8 +51,18 @@ def tile_list_crystal_disagreement_scores_kernel(
         w1_sc = [keep.tile([P, H], U8, name=f"w1_sc{a}", align_bytes=64) for a in range(PASSES)]
         w3_bf = keep.tile([P, PACK * N], BF16, name="w3_bf", align_bytes=64)
         w3_sc = keep.tile([P, N], U8, name="w3_sc", align_bytes=64)
-        h_slots = [keep.tile([P, PACK, 256], F32, name=f"h_slot{i}") for i in range(3)]
-        h_slot_of = {0: 0, 256: 1, 512: 2, 768: 0, 896: 2}
+        h_first = keep.tile([P, PACK, HALF], F32, name="h_first")
+        h_third = keep.tile([P, PACK, 256], F32, name="h_third")
+
+        def h_f32(lo, hi):
+            if lo < 512:
+                return h_first[:, :, lo:hi]
+            if lo < 768:
+                return h_third[:, :, lo - 512 : hi - 512]
+            if lo < 896:
+                return h_first[:, :, lo - 768 : hi - 768]
+            return h_third[:, :, lo - 896 : hi - 896]
+
         h_bf = keep.tile([P, S * PACK], BF16, name="h_bf", align_bytes=64)
         hq = keep.tile([P, S], U32, name="hq", align_bytes=64)
         h_sc = keep.tile([P, S], U8, name="h_sc", align_bytes=64)
@@ -145,7 +155,7 @@ def tile_list_crystal_disagreement_scores_kernel(
         tanh_a = [keep.tile([P, HALF], F32, name=f"tanh_a{u}") for u in range(8)]
         tanh_b = [keep.tile([P, HALF], F32, name=f"tanh_b{u}") for u in range(8)]
         sq_first = [keep.tile([P, HALF], F32, name=f"sq{t}")[:] for t in range(PACK - 1)]
-        sq_first.append(h_slots[2][:].rearrange("p t c -> p (t c)")[:, P : P + HALF])
+        sq_first.append(h_third[:].rearrange("p t c -> p (t c)")[:, P : P + HALF])
         sq_second = keep.tile([P, PACK, HALF], F32, name="sq_second")
         w3q = keep.tile([P, N], U32, name="w3q", align_bytes=64)
         banks = [psum.tile([P, HALF], F32, name=f"bank{i}") for i in range(8)]
@@ -209,21 +219,23 @@ def tile_list_crystal_disagreement_scores_kernel(
         def weigh(t, lo, hi):
             sq = sq_first[t][:, lo:hi] if lo < HALF else sq_second[:, t, lo - HALF : hi - HALF]
             nc.vector.tensor_tensor(
-                h_slots[h_slot_of[lo]][:, t, 0 : hi - lo], g_tab[t][:].indirect(listed(lo, hi)), sq, ALU.mult
+                h_f32(lo, hi)[:, t, :], g_tab[t][:].indirect(listed(lo, hi)), sq, ALU.mult
             )
 
         def interleave_h(engine_copy, lo, hi):
             engine_copy(
                 h_bf[:, lo * PACK : hi * PACK].rearrange("p (c i t) -> p c t i", i=4, t=PACK),
-                h_slots[h_slot_of[lo]][:, :, 0 : hi - lo].rearrange("p t (c i) -> p c t i", i=4),
+                h_f32(lo, hi).rearrange("p t (c i) -> p c t i", i=4),
             )
 
         out_view = out.rearrange("(b p) j -> p b j", p=P)
 
-        def read_out(o, lo, hi, engine_copy, queue):
+        def quantize_h(lo, hi):
             nc.vector.quantize_mx(
                 out=hq[:, lo:hi].bitcast(FP8X4), scales=h_sc[:, lo:hi], in_=h_bf[:, lo * PACK : hi * PACK]
             )
+
+        def read_out(o, lo, hi, engine_copy, queue):
             bank = banks[o][:, 0 : (N // P) * (hi - lo)].rearrange("p (b j) -> p b j", b=N // P)
             for b in range(N // P):
                 nc.tensor.matmul_mx(
@@ -251,9 +263,8 @@ def tile_list_crystal_disagreement_scores_kernel(
             head_a(t)
         for t in range(PACK):
             squared_difference(t)
-        weigh_first_half(0)
-        weigh_first_half(1)
-        weigh_first_half(2)
+        for t in range(PACK - 1):
+            weigh(t, 0, HALF)
         block_a(0)
         block_a(1)
         block_b(2)
@@ -269,20 +280,30 @@ def tile_list_crystal_disagreement_scores_kernel(
         )
         weigh_first_half(3)
         nc.vector.quantize_mx(out=w3q[:].bitcast(FP8X4), scales=w3_sc[:], in_=w3_bf[:])
-        interleave_h(nc.scalar.copy, 0, 256)
+        interleave_h(nc.vector.tensor_copy, 0, 256)
         block_square(3)
         interleave_h(nc.scalar.copy, 256, 512)
         for t in range(PACK):
             weigh(t, 512, 768)
         interleave_h(nc.scalar.copy, 512, 768)
+        quantize_h(0, 256)
         read_out(4, 0, 256, nc.scalar.copy, nc.sync)
         for t in range(PACK):
             weigh(t, 768, 896)
         interleave_h(nc.scalar.copy, 768, 896)
+        quantize_h(256, 512)
+        quantize_h(512, 768)
+        quantize_h(768, 896)
         read_out(5, 256, 512, nc.scalar.copy, nc.sync)
         read_out(2, 512, 768, nc.scalar.copy, nc.sync)
-        for t in range(PACK):
+        for t in range(PACK - 1):
             weigh(t, 896, 1024)
-        interleave_h(nc.vector.tensor_copy, 896, 1024)
+        weigh(PACK - 1, 896, 960)
+        weigh(PACK - 1, 960, 1024)
+        interleave_h(nc.vector.tensor_copy, 896, 960)
+        interleave_h(nc.vector.tensor_copy, 960, 1024)
+        quantize_h(896, 960)
+        quantize_h(960, 1024)
         read_out(3, 768, 896, nc.scalar.copy, nc.sync)
-        read_out(4, 896, 1024, nc.vector.tensor_copy, nc.scalar)
+        read_out(0, 896, 960, nc.scalar.copy, nc.sync)
+        read_out(1, 960, 1024, nc.vector.tensor_copy, nc.scalar)

@@ -52,16 +52,16 @@ def tile_list_crystal_disagreement_scores_kernel(
         w3_bf = keep.tile([P, PACK * N], BF16, name="w3_bf", align_bytes=64)
         w3_sc = keep.tile([P, N], U8, name="w3_sc", align_bytes=64)
         h_first = keep.tile([P, PACK, HALF], F32, name="h_first")
-        h_third = keep.tile([P, PACK, 256], F32, name="h_third")
+        h_block = [keep.tile([P, PACK, P], F32, name=f"h_block{i}") for i in range(2)]
 
         def h_f32(lo, hi):
             if lo < 512:
                 return h_first[:, :, lo:hi]
             if lo < 768:
-                return h_third[:, :, lo - 512 : hi - 512]
+                return h_block[(lo - 512) // P][:]
             if lo < 896:
                 return h_first[:, :, lo - 768 : hi - 768]
-            return h_third[:, :, lo - 896 : hi - 896]
+            return h_block[1][:, :, lo - 896 : hi - 896]
 
         h_bf = keep.tile([P, S * PACK], BF16, name="h_bf", align_bytes=64)
         hq = keep.tile([P, S], U32, name="hq", align_bytes=64)
@@ -154,8 +154,8 @@ def tile_list_crystal_disagreement_scores_kernel(
 
         tanh_a = [keep.tile([P, HALF], F32, name=f"tanh_a{u}") for u in range(8)]
         tanh_b = [keep.tile([P, HALF], F32, name=f"tanh_b{u}") for u in range(8)]
-        sq_first = [keep.tile([P, HALF], F32, name=f"sq{t}")[:] for t in range(PACK - 1)]
-        sq_first.append(h_third[:].rearrange("p t c -> p (t c)")[:, P : P + HALF])
+        sq_first = [keep.tile([P, HALF], F32, name=f"sq{t}")[:] for t in range(2)]
+        sq_first.extend(block[:].rearrange("p t c -> p (t c)") for block in h_block)
         sq_second = keep.tile([P, PACK, HALF], F32, name="sq_second")
         w3q = keep.tile([P, N], U32, name="w3q", align_bytes=64)
         banks = [psum.tile([P, HALF], F32, name=f"bank{i}") for i in range(8)]
@@ -192,8 +192,10 @@ def tile_list_crystal_disagreement_scores_kernel(
             passes(banks[4 + t], w1_cols(t * P, (t + 1) * P), tokens(0, HALF))
             nc.scalar.activation(tanh_a[t][:], banks[4 + t][:], ACT.Tanh)
 
-        def squared_difference(t):
+        def difference(t):
             nc.vector.tensor_tensor(sq_first[t], tanh_a[t][:], tanh_b[t][:], ALU.subtract)
+
+        def square(t):
             nc.scalar.activation(sq_first[t], sq_first[t], ACT.Square)
 
         def block_b(j):
@@ -262,15 +264,19 @@ def tile_list_crystal_disagreement_scores_kernel(
         for t in range(PACK):
             head_a(t)
         for t in range(PACK):
-            squared_difference(t)
+            difference(t)
+        square(0)
+        block_a(0)
+        square(1)
+        block_a(1)
+        square(2)
         for t in range(PACK - 1):
             weigh(t, 0, HALF)
-        block_a(0)
-        block_a(1)
-        block_b(2)
-        block_a(2)
         block_square(0)
         block_square(1)
+        square(3)
+        block_b(2)
+        block_a(2)
         block_b(3)
         block_a(3)
         block_square(2)
@@ -284,8 +290,11 @@ def tile_list_crystal_disagreement_scores_kernel(
         block_square(3)
         interleave_h(nc.scalar.copy, 256, 512)
         for t in range(PACK):
-            weigh(t, 512, 768)
-        interleave_h(nc.scalar.copy, 512, 768)
+            weigh(t, 512, 640)
+        interleave_h(nc.scalar.copy, 512, 640)
+        for t in range(PACK):
+            weigh(t, 640, 768)
+        interleave_h(nc.scalar.copy, 640, 768)
         quantize_h(0, 256)
         read_out(4, 0, 256, nc.scalar.copy, nc.sync)
         for t in range(PACK):

@@ -20,8 +20,14 @@ ALU = mybir.AluOpType
 P = 128
 PACK = 4
 PASSES = K // (P * PACK)
+QUADRANT = 32
+SCALE_ROWS = 4
+LIST_ROWS = 16
 HALF = S // 2
-MOVED_ROWS = 112
+CHUNK = 2 * P
+TAIL = P // 2
+RUN = 4
+MOVED_ROWS = P - QUADRANT + SCALE_ROWS
 
 
 def tile_list_crystal_disagreement_scores_kernel(
@@ -32,68 +38,70 @@ def tile_list_crystal_disagreement_scores_kernel(
         keep = ctx.enter_context(tc.tile_pool(name="keep", bufs=1))
         psum = ctx.enter_context(tc.psum_pool(name="psum", bufs=1))
 
-        offsets = keep.tile([P, S // 16], U16, name="offsets")
-        tab = [keep.tile([P, T], I32, name=f"tab{a}") for a in range(PASSES)]
-        w1_raw = [keep.tile([P, PACK, H], F32, name=f"w1_raw{a}") for a in range(PASSES)]
+        offsets = keep.tile([P, S // LIST_ROWS], U16, name="offsets")
+        tab = [keep.tile([P, T], I32, name=f"tab{g}") for g in range(PASSES)]
+        w1_raw = [keep.tile([P, PACK, H], F32, name=f"w1_raw{g}") for g in range(PASSES)]
         g_tab = [keep.tile([P, T], F32, name=f"g_tab{t}") for t in range(PACK)]
         w3_raw = keep.tile([P, PACK, N], F32, name="w3_raw")
         tab_sc = keep.tile([P, T // 4], I32, name="tab_sc")
         w2_raw = keep.tile([P, PASSES, H // 2], I32, name="w2_raw")
         w2_sc_raw = keep.tile([P, PASSES, H // 4], I32, name="w2_sc_raw")
 
-        v = [keep.tile([P, S], U32, name=f"v{a}", align_bytes=64) for a in range(PASSES)]
+        v = [keep.tile([P, S], U32, name=f"v{g}", align_bytes=64) for g in range(PASSES)]
         v_sc0 = keep.tile([P, S], U8, name="v_sc0", align_bytes=64)
-        v_sc_moved = [keep.tile([P, S // 4], I32, name=f"v_sc_moved{a}", align_bytes=64) for a in range(1, PASSES)]
+        v_sc_moved = [keep.tile([P, S // 4], I32, name=f"v_sc_moved{g}", align_bytes=64) for g in range(1, PASSES)]
         w2q = keep.tile([P, PASSES, H // 2], I32, name="w2q", align_bytes=64)
         w2_sc = keep.tile([P, PASSES, H // 4], I32, name="w2_sc", align_bytes=64)
-        w1_bf = [keep.tile([P, PACK * H], BF16, name=f"w1_bf{a}", align_bytes=64) for a in range(PASSES)]
-        w1q = [keep.tile([P, H], U32, name=f"w1q{a}", align_bytes=64) for a in range(PASSES)]
-        w1_sc = [keep.tile([P, H], U8, name=f"w1_sc{a}", align_bytes=64) for a in range(PASSES)]
+        w1_bf = [keep.tile([P, PACK * H], BF16, name=f"w1_bf{g}", align_bytes=64) for g in range(PASSES)]
+        w1q = [keep.tile([P, H], U32, name=f"w1q{g}", align_bytes=64) for g in range(PASSES)]
+        w1_sc = [keep.tile([P, H], U8, name=f"w1_sc{g}", align_bytes=64) for g in range(PASSES)]
         w3_bf = keep.tile([P, PACK * N], BF16, name="w3_bf", align_bytes=64)
         w3_sc = keep.tile([P, N], U8, name="w3_sc", align_bytes=64)
+
         h_first = keep.tile([P, PACK, HALF], F32, name="h_first")
         h_block = [keep.tile([P, PACK, P], F32, name=f"h_block{i}") for i in range(2)]
+        h_of_block = (h_block[0], h_block[1], h_first, h_block[1])
 
         def h_f32(lo, hi):
-            if lo < 512:
+            if lo < HALF:
                 return h_first[:, :, lo:hi]
-            if lo < 768:
-                return h_block[(lo - 512) // P][:]
-            if lo < 896:
-                return h_first[:, :, lo - 768 : hi - 768]
-            return h_block[1][:, :, lo - 896 : hi - 896]
+            j = (lo - HALF) // P
+            return h_of_block[j][:, :, lo - HALF - j * P : hi - HALF - j * P]
 
         h_bf = keep.tile([P, S * PACK], BF16, name="h_bf", align_bytes=64)
         hq = keep.tile([P, S], U32, name="hq", align_bytes=64)
         h_sc = keep.tile([P, S], U8, name="h_sc", align_bytes=64)
 
         def listed(lo, hi):
-            return offsets[:, lo // 16 : hi // 16]
+            return offsets[:, lo // LIST_ROWS : hi // LIST_ROWS]
 
-        def load_tab(a):
-            nc.sync.dma_start(tab[a][:], tab_words[a].rearrange("p n i -> p (n i)").bitcast(I32))
+        def load_tab(g):
+            nc.sync.dma_start(tab[g][:], tab_words[g].rearrange("p n i -> p (n i)").bitcast(I32))
 
         def load_tab_scales(queue, q):
-            queue.dma_start(tab_sc[32 * q : 32 * q + 4 * PASSES, :], tab_scales[:, 4 * q : 4 * q + 4, :].bitcast(I32))
-
-        def load_w1(a):
-            rows = w1[a * P * PACK : (a + 1) * P * PACK, :]
-            nc.sync.dma_start(w1_raw[a][:], rows.rearrange("(p j) c -> p j c", j=PACK))
-
-        def gather_words(a, lo, hi):
-            nc.vector.tensor_copy(v[a][:, lo:hi], tab[a][:].bitcast(U32).indirect(listed(lo, hi)))
-
-        def interleave_w1(engine_copy, a, t0, t1):
-            engine_copy(
-                w1_bf[a][:].rearrange("p (t m j) -> p m j t", t=PACK, j=PACK)[:, :, :, t0:t1],
-                w1_raw[a][:].rearrange("p j (m t) -> p m j t", t=PACK)[:, :, :, t0:t1],
+            queue.dma_start(
+                tab_sc[QUADRANT * q : QUADRANT * q + SCALE_ROWS * PASSES, :],
+                tab_scales[:, SCALE_ROWS * q : SCALE_ROWS * (q + 1), :].bitcast(I32),
             )
 
-        def quantize_w1(a, t0, t1):
+        def load_w1(g):
+            rows = w1[g * P * PACK : (g + 1) * P * PACK, :]
+            nc.sync.dma_start(w1_raw[g][:], rows.rearrange("(p i) c -> p i c", i=PACK))
+
+        def gather_words(g, lo, hi):
+            nc.vector.tensor_copy(v[g][:, lo:hi], tab[g][:].bitcast(U32).indirect(listed(lo, hi)))
+
+        def interleave_w1(engine_copy, g, t0, t1):
+            engine_copy(
+                w1_bf[g][:].rearrange("p (t m i) -> p m i t", t=PACK, i=PACK)[:, :, :, t0:t1],
+                w1_raw[g][:].rearrange("p i (m t) -> p m i t", t=PACK)[:, :, :, t0:t1],
+            )
+
+        def quantize_w1(g, t0, t1):
             nc.vector.quantize_mx(
-                out=w1q[a][:, t0 * P : t1 * P].bitcast(FP8X4),
-                scales=w1_sc[a][:, t0 * P : t1 * P],
-                in_=w1_bf[a][:, t0 * P * PACK : t1 * P * PACK],
+                out=w1q[g][:, t0 * P : t1 * P].bitcast(FP8X4),
+                scales=w1_sc[g][:, t0 * P : t1 * P],
+                in_=w1_bf[g][:, t0 * P * PACK : t1 * P * PACK],
             )
 
         nc.gpsimd.memset(tab_sc[:], 0)
@@ -102,6 +110,7 @@ def tile_list_crystal_disagreement_scores_kernel(
         make_identity(nc, ident[:])
         for moved in v_sc_moved:
             nc.vector.memset(moved[:], 0)
+
         nc.sync.dma_start(offsets[:], offs)
         load_tab(0)
         load_tab_scales(nc.scalar, 2)
@@ -109,79 +118,84 @@ def tile_list_crystal_disagreement_scores_kernel(
         load_tab_scales(nc.sync, 0)
         load_tab_scales(nc.sync, 1)
         load_w1(0)
-        nc.sync.dma_start(w2_raw[:], w2_words.rearrange("a p c -> p a c").bitcast(I32))
-        for q in range(4):
+        nc.sync.dma_start(w2_raw[:], w2_words.rearrange("g p c -> p g c").bitcast(I32))
+        for q in range(P // QUADRANT):
             nc.sync.dma_start(
-                w2_sc_raw[32 * q : 32 * q + 4, :, :],
-                w2_scales[:, 4 * q : 4 * q + 4, :].rearrange("a r c -> r a c").bitcast(I32),
+                w2_sc_raw[QUADRANT * q : QUADRANT * q + SCALE_ROWS, :, :],
+                w2_scales[:, SCALE_ROWS * q : SCALE_ROWS * (q + 1), :].rearrange("g s c -> s g c").bitcast(I32),
             )
         load_tab(1)
         load_tab(2)
 
         gather_words(0, 0, S)
         nc.vector.tensor_copy(v_sc0[:], tab_sc[:].bitcast(U8).indirect(offsets[:]))
-        for a in range(1, PASSES):
-            nc.sync.dma_start(v_sc_moved[a - 1][0:MOVED_ROWS, :], v_sc0[4 * a : 4 * a + MOVED_ROWS, :].bitcast(I32))
+        for g in range(1, PASSES):
+            nc.sync.dma_start(
+                v_sc_moved[g - 1][0:MOVED_ROWS, :], v_sc0[SCALE_ROWS * g : SCALE_ROWS * g + MOVED_ROWS, :].bitcast(I32)
+            )
         v_sc = [v_sc0[:]] + [moved[:].bitcast(U8) for moved in v_sc_moved]
 
         load_w1(1)
         load_w1(2)
         g_rows = gT.rearrange("(p t) n -> p t n", t=PACK)
-        nc.sync.dma_start(w3_raw[:], w3.rearrange("(p j) c -> p j c", j=PACK))
+        nc.sync.dma_start(w3_raw[:], w3.rearrange("(p t) n -> p t n", t=PACK))
         for t in range(PACK):
             nc.sync.dma_start(g_tab[t][:], g_rows[:, t, :])
 
         nc.vector.tensor_copy(
-            w2q[:].bitcast(U16).rearrange("p a (t m) -> p t a m", t=PACK),
-            w2_raw[:].bitcast(U16).rearrange("p a (m t) -> p t a m", t=PACK),
+            w2q[:].bitcast(U16).rearrange("p g (t m) -> p t g m", t=PACK),
+            w2_raw[:].bitcast(U16).rearrange("p g (m t) -> p t g m", t=PACK),
         )
         nc.vector.tensor_copy(
-            w2_sc[:].bitcast(U8).rearrange("p a (t m) -> p t a m", t=PACK),
-            w2_sc_raw[:].bitcast(U8).rearrange("p a (m t) -> p t a m", t=PACK),
+            w2_sc[:].bitcast(U8).rearrange("p g (t m) -> p t g m", t=PACK),
+            w2_sc_raw[:].bitcast(U8).rearrange("p g (m t) -> p t g m", t=PACK),
         )
-        interleave_w1(nc.scalar.copy, 0, 0, 2)
-        interleave_w1(nc.scalar.copy, 0, 2, 4)
+        interleave_w1(nc.scalar.copy, 0, 0, PACK // 2)
+        interleave_w1(nc.scalar.copy, 0, PACK // 2, PACK)
         quantize_w1(0, 0, PACK)
-        gather_words(1, 0, HALF)
-        gather_words(1, HALF, S)
-        gather_words(2, 0, HALF)
-        gather_words(2, HALF, S)
-        for a in range(1, PASSES):
-            interleave_w1(nc.vector.tensor_copy, a, 0, 2)
-            interleave_w1(nc.vector.tensor_copy, a, 2, 4)
-            quantize_w1(a, 0, 2)
-            quantize_w1(a, 2, 4)
+        for g in range(1, PASSES):
+            gather_words(g, 0, HALF)
+            gather_words(g, HALF, S)
+        for g in range(1, PASSES):
+            interleave_w1(nc.vector.tensor_copy, g, 0, PACK // 2)
+            interleave_w1(nc.vector.tensor_copy, g, PACK // 2, PACK)
+            quantize_w1(g, 0, PACK // 2)
+            quantize_w1(g, PACK // 2, PACK)
 
-        tanh_a = [keep.tile([P, HALF], F32, name=f"tanh_a{u}") for u in range(8)]
-        tanh_b = [keep.tile([P, HALF], F32, name=f"tanh_b{u}") for u in range(8)]
+        tanh_a = [keep.tile([P, HALF], F32, name=f"tanh_a{u}") for u in range(2 * PACK)]
+        tanh_b = [keep.tile([P, HALF], F32, name=f"tanh_b{u}") for u in range(2 * PACK)]
         sq_first = [keep.tile([P, HALF], F32, name=f"sq{t}")[:] for t in range(2)]
         sq_first.extend(block[:].rearrange("p t c -> p (t c)") for block in h_block)
         sq_second = keep.tile([P, PACK, HALF], F32, name="sq_second")
         w3q = keep.tile([P, N], U32, name="w3q", align_bytes=64)
-        banks = [psum.tile([P, HALF], F32, name=f"bank{i}") for i in range(8)]
+
+        banks = [psum.tile([P, HALF], F32, name=f"bank{i}") for i in range(2 * PACK)]
+        block_b_bank = (0, 1, 6, 7)
+        block_a_bank = (4, 5, 4, 5)
+        difference_bank = (2, 3, 0, 1)
 
         def passes(bank, stationary, moving):
-            for a in range(PASSES):
+            for g in range(PASSES):
                 nc.tensor.matmul_mx(
                     out=bank[:],
-                    lhsT=stationary(a)[0],
-                    lhsT_scale=stationary(a)[1],
-                    rhs=moving(a)[0],
-                    rhs_scale=moving(a)[1],
-                    start=(a == 0),
-                    stop=(a == PASSES - 1),
+                    lhsT=stationary(g)[0],
+                    lhsT_scale=stationary(g)[1],
+                    rhs=moving(g)[0],
+                    rhs_scale=moving(g)[1],
+                    start=(g == 0),
+                    stop=(g == PASSES - 1),
                 )
 
         def tokens(lo, hi):
-            return lambda a: (v[a][:, lo:hi].bitcast(FP8X4), v_sc[a][:, lo:hi])
+            return lambda g: (v[g][:, lo:hi].bitcast(FP8X4), v_sc[g][:, lo:hi])
 
         def w1_cols(lo, hi):
-            return lambda a: (w1q[a][:, lo:hi].bitcast(FP8X4), w1_sc[a][:, lo:hi])
+            return lambda g: (w1q[g][:, lo:hi].bitcast(FP8X4), w1_sc[g][:, lo:hi])
 
         def w2_cols(lo, hi):
-            return lambda a: (
-                w2q[:, a, :].bitcast(U8)[:, 2 * lo : 2 * hi].bitcast(FP4X4),
-                w2_sc[:, a, :].bitcast(U8)[:, lo:hi],
+            return lambda g: (
+                w2q[:, g, :].bitcast(U8)[:, 2 * lo : 2 * hi].bitcast(FP4X4),
+                w2_sc[:, g, :].bitcast(U8)[:, lo:hi],
             )
 
         def head_b(t):
@@ -189,8 +203,8 @@ def tile_list_crystal_disagreement_scores_kernel(
             nc.scalar.activation(tanh_b[t][:], banks[t][:], ACT.Tanh)
 
         def head_a(t):
-            passes(banks[4 + t], w1_cols(t * P, (t + 1) * P), tokens(0, HALF))
-            nc.scalar.activation(tanh_a[t][:], banks[4 + t][:], ACT.Tanh)
+            passes(banks[PACK + t], w1_cols(t * P, (t + 1) * P), tokens(0, HALF))
+            nc.scalar.activation(tanh_a[t][:], banks[PACK + t][:], ACT.Tanh)
 
         def difference(t):
             nc.vector.tensor_tensor(sq_first[t], tanh_a[t][:], tanh_b[t][:], ALU.subtract)
@@ -199,36 +213,38 @@ def tile_list_crystal_disagreement_scores_kernel(
             nc.scalar.activation(sq_first[t], sq_first[t], ACT.Square)
 
         def block_b(j):
-            bank = banks[(0, 1, 4, 5)[j]]
+            bank = banks[block_b_bank[j]]
             passes(bank, tokens(HALF + j * P, HALF + (j + 1) * P), w2_cols(0, H))
-            nc.scalar.activation(tanh_b[4 + j][:], bank[:], ACT.Tanh, scale=-1.0)
+            nc.scalar.activation(tanh_b[PACK + j][:], bank[:], ACT.Tanh, scale=-1.0)
 
         def block_a(j):
-            bank = banks[(6, 7, 6, 7)[j]]
+            bank = banks[block_a_bank[j]]
             passes(bank, tokens(HALF + j * P, HALF + (j + 1) * P), w1_cols(0, H))
-            nc.scalar.activation(tanh_a[4 + j][:], bank[:], ACT.Tanh)
+            nc.scalar.activation(tanh_a[PACK + j][:], bank[:], ACT.Tanh)
 
         def block_square(j):
-            bank = banks[(2, 3, 0, 1)[j]]
+            bank = banks[difference_bank[j]]
             for t in range(PACK):
                 cols = slice(t * P, (t + 1) * P)
-                nc.tensor.matmul(bank[:, cols], tanh_a[4 + j][:, cols], ident[:], start=True, stop=False, is_transpose=True)
-                nc.tensor.matmul(bank[:, cols], tanh_b[4 + j][:, cols], ident[:], start=False, stop=True, is_transpose=True)
+                for values, first in ((tanh_a[PACK + j], True), (tanh_b[PACK + j], False)):
+                    nc.tensor.matmul(
+                        bank[:, cols], values[:, cols], ident[:], start=first, stop=not first, is_transpose=True
+                    )
             nc.scalar.activation(
                 sq_second[:, :, j * P : (j + 1) * P], bank[:].rearrange("p (t c) -> p t c", t=PACK), ACT.Square
             )
 
         def weigh(t, lo, hi):
             sq = sq_first[t][:, lo:hi] if lo < HALF else sq_second[:, t, lo - HALF : hi - HALF]
-            nc.vector.tensor_tensor(
-                h_f32(lo, hi)[:, t, :], g_tab[t][:].indirect(listed(lo, hi)), sq, ALU.mult
+            nc.vector.tensor_tensor(h_f32(lo, hi)[:, t, :], g_tab[t][:].indirect(listed(lo, hi)), sq, ALU.mult)
+
+        def interleave(engine_copy, words, planes):
+            engine_copy(
+                words.rearrange("p (c e t) -> p c t e", e=RUN, t=PACK), planes.rearrange("p t (c e) -> p c t e", e=RUN)
             )
 
         def interleave_h(engine_copy, lo, hi):
-            engine_copy(
-                h_bf[:, lo * PACK : hi * PACK].rearrange("p (c i t) -> p c t i", i=4, t=PACK),
-                h_f32(lo, hi).rearrange("p t (c i) -> p c t i", i=4),
-            )
+            interleave(engine_copy, h_bf[:, lo * PACK : hi * PACK], h_f32(lo, hi))
 
         out_view = out.rearrange("(b p) j -> p b j", p=P)
 
@@ -237,8 +253,8 @@ def tile_list_crystal_disagreement_scores_kernel(
                 out=hq[:, lo:hi].bitcast(FP8X4), scales=h_sc[:, lo:hi], in_=h_bf[:, lo * PACK : hi * PACK]
             )
 
-        def read_out(o, lo, hi, engine_copy, queue):
-            bank = banks[o][:, 0 : (N // P) * (hi - lo)].rearrange("p (b j) -> p b j", b=N // P)
+        def read_out(bank_index, lo, hi, engine_copy, queue):
+            bank = banks[bank_index][:, 0 : (N // P) * (hi - lo)].rearrange("p (b j) -> p b j", b=N // P)
             for b in range(N // P):
                 nc.tensor.matmul_mx(
                     out=bank[:, b, :],
@@ -253,9 +269,13 @@ def tile_list_crystal_disagreement_scores_kernel(
             engine_copy(res[:], bank[:])
             queue.dma_start(out_view[:, :, lo:hi], res[:])
 
-        def weigh_first_half(t):
-            weigh(t, 0, 256)
-            weigh(t, 256, 512)
+        def block_tokens(j):
+            return HALF + j * P, HALF + (j + 1) * P
+
+        def weigh_block(j):
+            for t in range(PACK):
+                weigh(t, *block_tokens(j))
+            interleave_h(nc.scalar.copy, *block_tokens(j))
 
         for t in range(PACK):
             head_b(t)
@@ -274,45 +294,38 @@ def tile_list_crystal_disagreement_scores_kernel(
             weigh(t, 0, HALF)
         block_square(0)
         block_square(1)
-        square(3)
-        block_b(2)
-        block_a(2)
-        block_b(3)
-        block_a(3)
+        square(PACK - 1)
+        for j in (2, 3):
+            block_b(j)
+            block_a(j)
         block_square(2)
-        nc.vector.tensor_copy(
-            w3_bf[:].rearrange("p (c i j) -> p c j i", i=4, j=PACK),
-            w3_raw[:].rearrange("p j (c i) -> p c j i", i=4),
-        )
-        weigh_first_half(3)
+        interleave(nc.vector.tensor_copy, w3_bf[:], w3_raw[:])
+        weigh(PACK - 1, 0, CHUNK)
+        weigh(PACK - 1, CHUNK, HALF)
         nc.vector.quantize_mx(out=w3q[:].bitcast(FP8X4), scales=w3_sc[:], in_=w3_bf[:])
-        interleave_h(nc.vector.tensor_copy, 0, 256)
+        interleave_h(nc.vector.tensor_copy, 0, P)
+        interleave_h(nc.scalar.copy, P, CHUNK)
         block_square(3)
-        interleave_h(nc.scalar.copy, 256, 512)
-        for t in range(PACK):
-            weigh(t, 512, 640)
-        interleave_h(nc.scalar.copy, 512, 640)
-        for t in range(PACK):
-            weigh(t, 640, 768)
-        interleave_h(nc.scalar.copy, 640, 768)
-        quantize_h(0, 256)
-        read_out(4, 0, 256, nc.scalar.copy, nc.sync)
-        for t in range(PACK):
-            weigh(t, 768, 896)
-        interleave_h(nc.scalar.copy, 768, 896)
-        quantize_h(256, 512)
-        quantize_h(512, 768)
-        quantize_h(768, 896)
-        read_out(5, 256, 512, nc.scalar.copy, nc.sync)
-        read_out(2, 512, 768, nc.scalar.copy, nc.sync)
+        interleave_h(nc.scalar.copy, CHUNK, HALF)
+        weigh_block(0)
+        weigh_block(1)
+        quantize_h(0, CHUNK)
+        read_out(6, 0, CHUNK, nc.scalar.copy, nc.sync)
+        weigh_block(2)
+        quantize_h(CHUNK, HALF)
+        quantize_h(HALF, HALF + CHUNK)
+        quantize_h(*block_tokens(2))
+        read_out(7, CHUNK, HALF, nc.scalar.copy, nc.sync)
+        read_out(2, HALF, HALF + CHUNK, nc.scalar.copy, nc.sync)
+        tails = ((S - P, S - TAIL), (S - TAIL, S))
         for t in range(PACK - 1):
-            weigh(t, 896, 1024)
-        weigh(PACK - 1, 896, 960)
-        weigh(PACK - 1, 960, 1024)
-        interleave_h(nc.vector.tensor_copy, 896, 960)
-        interleave_h(nc.vector.tensor_copy, 960, 1024)
-        quantize_h(896, 960)
-        quantize_h(960, 1024)
-        read_out(3, 768, 896, nc.scalar.copy, nc.sync)
-        read_out(0, 896, 960, nc.scalar.copy, nc.sync)
-        read_out(1, 960, 1024, nc.vector.tensor_copy, nc.scalar)
+            weigh(t, S - P, S)
+        for lo, hi in tails:
+            weigh(PACK - 1, lo, hi)
+        for lo, hi in tails:
+            interleave_h(nc.vector.tensor_copy, lo, hi)
+        for lo, hi in tails:
+            quantize_h(lo, hi)
+        read_out(3, *block_tokens(2), nc.scalar.copy, nc.sync)
+        read_out(0, *tails[0], nc.scalar.copy, nc.sync)
+        read_out(1, *tails[1], nc.vector.tensor_copy, nc.scalar)

@@ -27,7 +27,7 @@ HALF = S // 2
 CHUNK = 2 * P
 TAIL = P // 2
 RUN = 4
-MOVED_ROWS = P - QUADRANT + SCALE_ROWS
+PASS_ROWS = 16
 
 
 def tile_list_crystal_disagreement_scores_kernel(
@@ -48,8 +48,9 @@ def tile_list_crystal_disagreement_scores_kernel(
         w2_sc_raw = keep.tile([P, PASSES, H // 4], I32, name="w2_sc_raw")
 
         v = [keep.tile([P, S], U32, name=f"v{g}", align_bytes=64) for g in range(PASSES)]
-        v_sc0 = keep.tile([P, S], U8, name="v_sc0", align_bytes=64)
-        v_sc_moved = [keep.tile([P, S // 4], I32, name=f"v_sc_moved{g}", align_bytes=64) for g in range(1, PASSES)]
+        sc_rows = keep.tile([P, S], U8, name="sc_rows", align_bytes=64)
+        placed = [keep.tile([P, S // 4], I32, name=f"placed{g}", align_bytes=64) for g in range(PASSES)]
+        v_sc = [plane[:].bitcast(U8) for plane in placed]
         w2q = keep.tile([P, PASSES, H // 2], I32, name="w2q", align_bytes=64)
         w2_sc = keep.tile([P, PASSES, H // 4], I32, name="w2_sc", align_bytes=64)
         w1_bf = [keep.tile([P, PACK * H], BF16, name=f"w1_bf{g}", align_bytes=64) for g in range(PASSES)]
@@ -78,11 +79,13 @@ def tile_list_crystal_disagreement_scores_kernel(
         def load_tab(g):
             nc.sync.dma_start(tab[g][:], tab_words[g].rearrange("p n i -> p (n i)").bitcast(I32))
 
-        def load_tab_scales(queue, q):
-            queue.dma_start(
-                tab_sc[QUADRANT * q : QUADRANT * q + SCALE_ROWS * PASSES, :],
-                tab_scales[:, SCALE_ROWS * q : SCALE_ROWS * (q + 1), :].bitcast(I32),
-            )
+        def place_scale_rows(g):
+            for q in range(P // QUADRANT):
+                first = PASS_ROWS * g + SCALE_ROWS * q
+                nc.sync.dma_start(
+                    placed[g][QUADRANT * q : QUADRANT * q + SCALE_ROWS, :],
+                    sc_rows[first : first + SCALE_ROWS, :].bitcast(I32),
+                )
 
         def load_w1(g):
             rows = w1[g * P * PACK : (g + 1) * P * PACK, :]
@@ -104,36 +107,32 @@ def tile_list_crystal_disagreement_scores_kernel(
                 in_=w1_bf[g][:, t0 * P * PACK : t1 * P * PACK],
             )
 
-        nc.gpsimd.memset(tab_sc[:], 0)
-        nc.gpsimd.memset(w2_sc_raw[:], 0)
+        nc.gpsimd.memset(tab_sc[QUADRANT : 2 * QUADRANT, :], 0)
+        nc.gpsimd.memset(tab_sc[2 * QUADRANT :, :], 0)
+        nc.vector.memset(w2_sc_raw[:], 0)
         ident = keep.tile([P, P], F32, name="ident")
         make_identity(nc, ident[:])
-        for moved in v_sc_moved:
-            nc.vector.memset(moved[:], 0)
+        for plane in placed:
+            nc.vector.memset(plane[:], 0)
 
+        scale_rows = tab_scales.rearrange("g q n -> (g q) n").bitcast(I32)
         nc.sync.dma_start(offsets[:], offs)
+        nc.sync.dma_start(tab_sc[0:QUADRANT, :], scale_rows[0:QUADRANT, :])
+        nc.sync.dma_start(tab_sc[QUADRANT : QUADRANT + PASS_ROWS, :], scale_rows[QUADRANT:, :])
         load_tab(0)
-        load_tab_scales(nc.scalar, 2)
-        load_tab_scales(nc.scalar, 3)
-        load_tab_scales(nc.sync, 0)
-        load_tab_scales(nc.sync, 1)
-        load_w1(0)
-        nc.sync.dma_start(w2_raw[:], w2_words.rearrange("g p c -> p g c").bitcast(I32))
         for q in range(P // QUADRANT):
             nc.sync.dma_start(
                 w2_sc_raw[QUADRANT * q : QUADRANT * q + SCALE_ROWS, :, :],
                 w2_scales[:, SCALE_ROWS * q : SCALE_ROWS * (q + 1), :].rearrange("g s c -> s g c").bitcast(I32),
             )
-        load_tab(1)
-        load_tab(2)
-
+        load_w1(0)
+        nc.sync.dma_start(w2_raw[:], w2_words.rearrange("g p c -> p g c").bitcast(I32))
+        nc.vector.tensor_copy(sc_rows[:], tab_sc[:].bitcast(U8).indirect(offsets[:]))
         gather_words(0, 0, S)
-        nc.vector.tensor_copy(v_sc0[:], tab_sc[:].bitcast(U8).indirect(offsets[:]))
-        for g in range(1, PASSES):
-            nc.sync.dma_start(
-                v_sc_moved[g - 1][0:MOVED_ROWS, :], v_sc0[SCALE_ROWS * g : SCALE_ROWS * g + MOVED_ROWS, :].bitcast(I32)
-            )
-        v_sc = [v_sc0[:]] + [moved[:].bitcast(U8) for moved in v_sc_moved]
+        for g in range(PASSES):
+            place_scale_rows(g)
+            if g + 1 < PASSES:
+                load_tab(g + 1)
 
         load_w1(1)
         load_w1(2)

@@ -79,9 +79,9 @@ def tile_list_crystal_disagreement_scores_kernel(
         def load_tab(g):
             nc.sync.dma_start(tab[g][:], tab_words[g].rearrange("p n i -> p (n i)").bitcast(I32))
 
-        def place_scale_rows(g):
-            for q in range(P // QUADRANT):
-                first = PASS_ROWS * g + SCALE_ROWS * q
+        def place_scale_rows(moves):
+            for g, q in moves:
+                first = (2 * QUADRANT, 2 * QUADRANT + PASS_ROWS, P - PASS_ROWS)[g] + SCALE_ROWS * q
                 nc.sync.dma_start(
                     placed[g][QUADRANT * q : QUADRANT * q + SCALE_ROWS, :],
                     sc_rows[first : first + SCALE_ROWS, :].bitcast(I32),
@@ -107,8 +107,8 @@ def tile_list_crystal_disagreement_scores_kernel(
                 in_=w1_bf[g][:, t0 * P * PACK : t1 * P * PACK],
             )
 
-        nc.gpsimd.memset(tab_sc[QUADRANT : 2 * QUADRANT, :], 0)
-        nc.gpsimd.memset(tab_sc[2 * QUADRANT :, :], 0)
+        nc.gpsimd.memset(tab_sc[0 : 2 * QUADRANT, :], 0)
+        nc.gpsimd.memset(tab_sc[3 * QUADRANT : 3 * QUADRANT + PASS_ROWS, :], 0)
         nc.vector.memset(w2_sc_raw[:], 0)
         ident = keep.tile([P, P], F32, name="ident")
         make_identity(nc, ident[:])
@@ -117,23 +117,24 @@ def tile_list_crystal_disagreement_scores_kernel(
 
         scale_rows = tab_scales.rearrange("g q n -> (g q) n").bitcast(I32)
         nc.sync.dma_start(offsets[:], offs)
-        nc.sync.dma_start(tab_sc[0:QUADRANT, :], scale_rows[0:QUADRANT, :])
-        nc.sync.dma_start(tab_sc[QUADRANT : QUADRANT + PASS_ROWS, :], scale_rows[QUADRANT:, :])
+        nc.sync.dma_start(tab_sc[2 * QUADRANT : 3 * QUADRANT, :], scale_rows[0:QUADRANT, :])
+        nc.sync.dma_start(tab_sc[P - PASS_ROWS :, :], scale_rows[QUADRANT:, :])
         load_tab(0)
         for q in range(P // QUADRANT):
             nc.sync.dma_start(
                 w2_sc_raw[QUADRANT * q : QUADRANT * q + SCALE_ROWS, :, :],
                 w2_scales[:, SCALE_ROWS * q : SCALE_ROWS * (q + 1), :].rearrange("g s c -> s g c").bitcast(I32),
             )
-        load_w1(0)
         nc.sync.dma_start(w2_raw[:], w2_words.rearrange("g p c -> p g c").bitcast(I32))
+        load_tab(1)
         nc.vector.tensor_copy(sc_rows[:], tab_sc[:].bitcast(U8).indirect(offsets[:]))
         gather_words(0, 0, S)
-        for g in range(PASSES):
-            place_scale_rows(g)
-            if g + 1 < PASSES:
-                load_tab(g + 1)
-
+        moves = [(g, q) for g in range(PASSES) for q in range(P // QUADRANT)]
+        place_scale_rows(moves[:6])
+        load_tab(2)
+        place_scale_rows(moves[6:8])
+        load_w1(0)
+        place_scale_rows(moves[8:])
         load_w1(1)
         load_w1(2)
         g_rows = gT.rearrange("(p t) n -> p t n", t=PACK)
@@ -141,7 +142,7 @@ def tile_list_crystal_disagreement_scores_kernel(
         for t in range(PACK):
             nc.sync.dma_start(g_tab[t][:], g_rows[:, t, :])
 
-        nc.vector.tensor_copy(
+        nc.scalar.copy(
             w2q[:].bitcast(U16).rearrange("p g (t m) -> p t g m", t=PACK),
             w2_raw[:].bitcast(U16).rearrange("p g (m t) -> p t g m", t=PACK),
         )
@@ -149,12 +150,12 @@ def tile_list_crystal_disagreement_scores_kernel(
             w2_sc[:].bitcast(U8).rearrange("p g (t m) -> p t g m", t=PACK),
             w2_sc_raw[:].bitcast(U8).rearrange("p g (m t) -> p t g m", t=PACK),
         )
-        interleave_w1(nc.scalar.copy, 0, 0, PACK // 2)
-        interleave_w1(nc.scalar.copy, 0, PACK // 2, PACK)
-        quantize_w1(0, 0, PACK)
         for g in range(1, PASSES):
             gather_words(g, 0, HALF)
             gather_words(g, HALF, S)
+        interleave_w1(nc.scalar.copy, 0, 0, PACK // 2)
+        interleave_w1(nc.vector.tensor_copy, 0, PACK // 2, PACK)
+        quantize_w1(0, 0, PACK)
         for g in range(1, PASSES):
             interleave_w1(nc.vector.tensor_copy, g, 0, PACK // 2)
             interleave_w1(nc.vector.tensor_copy, g, PACK // 2, PACK)
@@ -162,16 +163,18 @@ def tile_list_crystal_disagreement_scores_kernel(
             quantize_w1(g, PACK // 2, PACK)
 
         tanh_a = [keep.tile([P, HALF], F32, name=f"tanh_a{u}") for u in range(2 * PACK)]
-        tanh_b = [keep.tile([P, HALF], F32, name=f"tanh_b{u}") for u in range(2 * PACK)]
+        tanh_b_first = keep.tile([P, PACK, HALF], F32, name="tanh_b_first")
+        tanh_b = [tanh_b_first[:, t, :] for t in range(PACK)]
+        tanh_b.extend(keep.tile([P, HALF], F32, name=f"tanh_b{u}")[:] for u in range(PACK))
         sq_first = [keep.tile([P, HALF], F32, name=f"sq{t}")[:] for t in range(2)]
         sq_first.extend(block[:].rearrange("p t c -> p (t c)") for block in h_block)
         sq_second = keep.tile([P, PACK, HALF], F32, name="sq_second")
         w3q = keep.tile([P, N], U32, name="w3q", align_bytes=64)
 
         banks = [psum.tile([P, HALF], F32, name=f"bank{i}") for i in range(2 * PACK)]
-        block_b_bank = (0, 1, 6, 7)
-        block_a_bank = (4, 5, 4, 5)
-        difference_bank = (2, 3, 0, 1)
+        block_b_bank = (4, 5, 6, 7)
+        block_a_bank = (0, 1, 2, 3)
+        difference_bank = (4, 5, 6, 7)
 
         def passes(bank, stationary, moving):
             for g in range(PASSES):
@@ -199,14 +202,14 @@ def tile_list_crystal_disagreement_scores_kernel(
 
         def head_b(t):
             passes(banks[t], w2_cols(t * P, (t + 1) * P), tokens(0, HALF))
-            nc.scalar.activation(tanh_b[t][:], banks[t][:], ACT.Tanh)
+            nc.scalar.activation(tanh_b[t], banks[t][:], ACT.Tanh)
 
         def head_a(t):
-            passes(banks[PACK + t], w1_cols(t * P, (t + 1) * P), tokens(0, HALF))
-            nc.scalar.activation(tanh_a[t][:], banks[PACK + t][:], ACT.Tanh)
+            passes(banks[t], w1_cols(t * P, (t + 1) * P), tokens(0, HALF))
+            nc.scalar.activation(tanh_a[t][:], banks[t][:], ACT.Tanh)
 
         def difference(t):
-            nc.vector.tensor_tensor(sq_first[t], tanh_a[t][:], tanh_b[t][:], ALU.subtract)
+            nc.vector.tensor_tensor(sq_first[t], tanh_a[t][:], tanh_b[t], ALU.subtract)
 
         def square(t):
             nc.scalar.activation(sq_first[t], sq_first[t], ACT.Square)
@@ -214,7 +217,7 @@ def tile_list_crystal_disagreement_scores_kernel(
         def block_b(j):
             bank = banks[block_b_bank[j]]
             passes(bank, tokens(HALF + j * P, HALF + (j + 1) * P), w2_cols(0, H))
-            nc.scalar.activation(tanh_b[PACK + j][:], bank[:], ACT.Tanh, scale=-1.0)
+            nc.scalar.activation(tanh_b[PACK + j], bank[:], ACT.Tanh, scale=-1.0)
 
         def block_a(j):
             bank = banks[block_a_bank[j]]
@@ -278,8 +281,8 @@ def tile_list_crystal_disagreement_scores_kernel(
 
         for t in range(PACK):
             head_b(t)
-        block_b(0)
-        block_b(1)
+        for j in range(PACK):
+            block_b(j)
         for t in range(PACK):
             head_a(t)
         for t in range(PACK):
@@ -295,7 +298,6 @@ def tile_list_crystal_disagreement_scores_kernel(
         block_square(1)
         square(PACK - 1)
         for j in (2, 3):
-            block_b(j)
             block_a(j)
         block_square(2)
         interleave(nc.vector.tensor_copy, w3_bf[:], w3_raw[:])
@@ -309,12 +311,12 @@ def tile_list_crystal_disagreement_scores_kernel(
         weigh_block(0)
         weigh_block(1)
         quantize_h(0, CHUNK)
-        read_out(6, 0, CHUNK, nc.scalar.copy, nc.sync)
+        read_out(0, 0, CHUNK, nc.scalar.copy, nc.sync)
         weigh_block(2)
         quantize_h(CHUNK, HALF)
         quantize_h(HALF, HALF + CHUNK)
         quantize_h(*block_tokens(2))
-        read_out(7, CHUNK, HALF, nc.scalar.copy, nc.sync)
+        read_out(1, CHUNK, HALF, nc.scalar.copy, nc.sync)
         read_out(2, HALF, HALF + CHUNK, nc.scalar.copy, nc.sync)
         tails = ((S - P, S - TAIL), (S - TAIL, S))
         for t in range(PACK - 1):
@@ -326,5 +328,5 @@ def tile_list_crystal_disagreement_scores_kernel(
         for lo, hi in tails:
             quantize_h(lo, hi)
         read_out(3, *block_tokens(2), nc.scalar.copy, nc.sync)
-        read_out(0, *tails[0], nc.scalar.copy, nc.sync)
-        read_out(1, *tails[1], nc.vector.tensor_copy, nc.scalar)
+        read_out(4, *tails[0], nc.scalar.copy, nc.sync)
+        read_out(5, *tails[1], nc.vector.tensor_copy, nc.scalar)

@@ -130,9 +130,9 @@ def tile_list_crystal_disagreement_scores_kernel(
         nc.vector.tensor_copy(sc_rows[:], tab_sc[:].bitcast(U8).indirect(offsets[:]))
         gather_words(0, 0, S)
         moves = [(g, q) for g in range(PASSES) for q in range(P // QUADRANT)]
-        place_scale_rows(moves[:6])
+        place_scale_rows(moves[:4])
         load_tab(2)
-        place_scale_rows(moves[6:8])
+        place_scale_rows(moves[4:8])
         load_w1(0)
         place_scale_rows(moves[8:])
         load_w1(1)

@@ -107,9 +107,9 @@ def tile_list_crystal_disagreement_scores_kernel(
                 in_=w1_bf[g][:, t0 * P * PACK : t1 * P * PACK],
             )
 
-        nc.gpsimd.memset(tab_sc[0 : 2 * QUADRANT, :], 0)
-        nc.gpsimd.memset(tab_sc[3 * QUADRANT : 3 * QUADRANT + PASS_ROWS, :], 0)
-        nc.vector.memset(w2_sc_raw[:], 0)
+        nc.gpsimd.memset(w2_sc_raw[:], 0)
+        nc.vector.memset(tab_sc[0 : 2 * QUADRANT, :], 0)
+        nc.vector.memset(tab_sc[3 * QUADRANT : 3 * QUADRANT + PASS_ROWS, :], 0)
         ident = keep.tile([P, P], F32, name="ident")
         make_identity(nc, ident[:])
         for plane in placed:
@@ -117,11 +117,11 @@ def tile_list_crystal_disagreement_scores_kernel(
 
         scale_rows = tab_scales.rearrange("g q n -> (g q) n").bitcast(I32)
         nc.sync.dma_start(offsets[:], offs)
-        nc.sync.dma_start(tab_sc[2 * QUADRANT : 3 * QUADRANT, :], scale_rows[0:QUADRANT, :])
+        nc.scalar.dma_start(tab_sc[2 * QUADRANT : 3 * QUADRANT, :], scale_rows[0:QUADRANT, :])
         nc.sync.dma_start(tab_sc[P - PASS_ROWS :, :], scale_rows[QUADRANT:, :])
         load_tab(0)
         for q in range(P // QUADRANT):
-            nc.sync.dma_start(
+            nc.scalar.dma_start(
                 w2_sc_raw[QUADRANT * q : QUADRANT * q + SCALE_ROWS, :, :],
                 w2_scales[:, SCALE_ROWS * q : SCALE_ROWS * (q + 1), :].rearrange("g s c -> s g c").bitcast(I32),
             )

@@ -146,7 +146,7 @@ def tile_list_crystal_disagreement_scores_kernel(
             w2q[:].bitcast(U16).rearrange("p g (t m) -> p t g m", t=PACK),
             w2_raw[:].bitcast(U16).rearrange("p g (m t) -> p t g m", t=PACK),
         )
-        nc.vector.tensor_copy(
+        nc.gpsimd.tensor_copy(
             w2_sc[:].bitcast(U8).rearrange("p g (t m) -> p t g m", t=PACK),
             w2_sc_raw[:].bitcast(U8).rearrange("p g (m t) -> p t g m", t=PACK),
         )

@@ -27,6 +27,7 @@ HALF = S // 2
 CHUNK = 2 * P
 TAIL = P // 2
 RUN = 4
+DMA_ALIGN = 256
 PASS_ROWS = 16
 
 
@@ -39,13 +40,13 @@ def tile_list_crystal_disagreement_scores_kernel(
         psum = ctx.enter_context(tc.psum_pool(name="psum", bufs=1))
 
         offsets = keep.tile([P, S // LIST_ROWS], U16, name="offsets")
-        tab = [keep.tile([P, T], I32, name=f"tab{g}") for g in range(PASSES)]
-        w1_raw = [keep.tile([P, PACK, H], F32, name=f"w1_raw{g}") for g in range(PASSES)]
-        g_tab = [keep.tile([P, T], F32, name=f"g_tab{t}") for t in range(PACK)]
-        w3_raw = keep.tile([P, PACK, N], F32, name="w3_raw")
-        tab_sc = keep.tile([P, T // 4], I32, name="tab_sc")
-        w2_raw = keep.tile([P, PASSES, H // 2], I32, name="w2_raw")
-        w2_sc_raw = keep.tile([P, PASSES, H // 4], I32, name="w2_sc_raw")
+        tab = [keep.tile([P, T], I32, name=f"tab{g}", align_bytes=DMA_ALIGN) for g in range(PASSES)]
+        w1_raw = [keep.tile([P, PACK, H], F32, name=f"w1_raw{g}", align_bytes=DMA_ALIGN) for g in range(PASSES)]
+        g_tab = [keep.tile([P, T], F32, name=f"g_tab{t}", align_bytes=DMA_ALIGN) for t in range(PACK)]
+        w3_raw = keep.tile([P, PACK, N], F32, name="w3_raw", align_bytes=DMA_ALIGN)
+        tab_sc = keep.tile([P, T // 4], I32, name="tab_sc", align_bytes=DMA_ALIGN)
+        w2_raw = keep.tile([P, PASSES, H // 2], I32, name="w2_raw", align_bytes=DMA_ALIGN)
+        w2_sc_raw = keep.tile([P, PASSES, H // 4], I32, name="w2_sc_raw", align_bytes=DMA_ALIGN)
 
         v = [keep.tile([P, S], U32, name=f"v{g}", align_bytes=64) for g in range(PASSES)]
         sc_rows = keep.tile([P, S], U8, name="sc_rows", align_bytes=64)
@@ -267,7 +268,7 @@ def tile_list_crystal_disagreement_scores_kernel(
                     start=True,
                     stop=True,
                 )
-            res = keep.tile([P, N // P, hi - lo], F32, name=f"res{lo}")
+            res = keep.tile([P, N // P, hi - lo], F32, name=f"res{lo}", align_bytes=DMA_ALIGN)
             engine_copy(res[:], bank[:])
             queue.dma_start(out_view[:, :, lo:hi], res[:])
 

@@ -329,5 +329,5 @@ def tile_list_crystal_disagreement_scores_kernel(
         for lo, hi in tails:
             quantize_h(lo, hi)
         read_out(3, *block_tokens(2), nc.scalar.copy, nc.sync)
-        read_out(4, *tails[0], nc.scalar.copy, nc.sync)
-        read_out(5, *tails[1], nc.vector.tensor_copy, nc.scalar)
+        read_out(4, *tails[0], nc.scalar.copy, nc.scalar)
+        read_out(5, *tails[1], nc.vector.tensor_copy, nc.sync)

@@ -329,5 +329,5 @@ def tile_list_crystal_disagreement_scores_kernel(
         for lo, hi in tails:
             quantize_h(lo, hi)
         read_out(3, *block_tokens(2), nc.scalar.copy, nc.sync)
-        read_out(4, *tails[0], nc.scalar.copy, nc.scalar)
+        read_out(4, *tails[0], nc.scalar.copy, nc.sync)
         read_out(5, *tails[1], nc.vector.tensor_copy, nc.sync)

@@ -50,8 +50,9 @@ def tile_list_crystal_disagreement_scores_kernel(
 
         v = [keep.tile([P, S], U32, name=f"v{g}", align_bytes=64) for g in range(PASSES)]
         sc_rows = keep.tile([P, S], U8, name="sc_rows", align_bytes=64)
-        placed = [keep.tile([P, S // 4], I32, name=f"placed{g}", align_bytes=64) for g in range(PASSES)]
-        v_sc = [plane[:].bitcast(U8) for plane in placed]
+        placed_pair = keep.tile([P, 2, S // 4], I32, name="placed_pair", align_bytes=64)
+        placed_last = keep.tile([P, S // 4], I32, name="placed_last", align_bytes=64)
+        v_sc = [placed_pair[:, 0, :].bitcast(U8), placed_pair[:, 1, :].bitcast(U8), placed_last[:].bitcast(U8)]
         w2q = keep.tile([P, PASSES, H // 2], I32, name="w2q", align_bytes=64)
         w2_sc = keep.tile([P, PASSES, H // 4], I32, name="w2_sc", align_bytes=64)
         w1_bf = [keep.tile([P, PACK * H], BF16, name=f"w1_bf{g}", align_bytes=64) for g in range(PASSES)]
@@ -80,11 +81,19 @@ def tile_list_crystal_disagreement_scores_kernel(
         def load_tab(g):
             nc.sync.dma_start(tab[g][:], tab_words[g].rearrange("p n i -> p (n i)").bitcast(I32))
 
-        def place_scale_rows(moves):
-            for g, q in moves:
-                first = (2 * QUADRANT, 2 * QUADRANT + PASS_ROWS, P - PASS_ROWS)[g] + SCALE_ROWS * q
+        def place_pair():
+            for q in range(P // QUADRANT):
+                first = 2 * QUADRANT + 2 * SCALE_ROWS * q
                 nc.sync.dma_start(
-                    placed[g][QUADRANT * q : QUADRANT * q + SCALE_ROWS, :],
+                    placed_pair[QUADRANT * q : QUADRANT * q + SCALE_ROWS, :, :],
+                    sc_rows[first : first + 2 * SCALE_ROWS, :].bitcast(I32),
+                )
+
+        def place_last():
+            for q in range(P // QUADRANT):
+                first = P - PASS_ROWS + SCALE_ROWS * q
+                nc.sync.dma_start(
+                    placed_last[QUADRANT * q : QUADRANT * q + SCALE_ROWS, :],
                     sc_rows[first : first + SCALE_ROWS, :].bitcast(I32),
                 )
 
@@ -113,13 +122,12 @@ def tile_list_crystal_disagreement_scores_kernel(
         nc.vector.memset(tab_sc[3 * QUADRANT : 3 * QUADRANT + PASS_ROWS, :], 0)
         ident = keep.tile([P, P], F32, name="ident")
         make_identity(nc, ident[:])
-        for plane in placed:
-            nc.vector.memset(plane[:], 0)
+        nc.vector.memset(placed_pair[:], 0)
+        nc.vector.memset(placed_last[:], 0)
 
-        scale_rows = tab_scales.rearrange("g q n -> (g q) n").bitcast(I32)
         nc.sync.dma_start(offsets[:], offs)
-        nc.scalar.dma_start(tab_sc[2 * QUADRANT : 3 * QUADRANT, :], scale_rows[0:QUADRANT, :])
-        nc.sync.dma_start(tab_sc[P - PASS_ROWS :, :], scale_rows[QUADRANT:, :])
+        nc.scalar.dma_start(tab_sc[2 * QUADRANT : 3 * QUADRANT, :], tab_scales[0:2].rearrange("g q n -> q g n").bitcast(I32))
+        nc.sync.dma_start(tab_sc[P - PASS_ROWS :, :], tab_scales[2].bitcast(I32))
         load_tab(0)
         for q in range(P // QUADRANT):
             nc.scalar.dma_start(
@@ -130,12 +138,10 @@ def tile_list_crystal_disagreement_scores_kernel(
         load_tab(1)
         nc.vector.tensor_copy(sc_rows[:], tab_sc[:].bitcast(U8).indirect(offsets[:]))
         gather_words(0, 0, S)
-        moves = [(g, q) for g in range(PASSES) for q in range(P // QUADRANT)]
-        place_scale_rows(moves[:4])
+        place_pair()
         load_tab(2)
-        place_scale_rows(moves[4:8])
+        place_last()
         load_w1(0)
-        place_scale_rows(moves[8:])
         load_w1(1)
         load_w1(2)
         g_rows = gT.rearrange("(p t) n -> p t n", t=PACK)
@@ -154,7 +160,7 @@ def tile_list_crystal_disagreement_scores_kernel(
         for g in range(1, PASSES):
             gather_words(g, 0, HALF)
             gather_words(g, HALF, S)
-        interleave_w1(nc.scalar.copy, 0, 0, PACK // 2)
+        interleave_w1(nc.vector.tensor_copy, 0, 0, PACK // 2)
         interleave_w1(nc.vector.tensor_copy, 0, PACK // 2, PACK)
         quantize_w1(0, 0, PACK)
         for g in range(1, PASSES):

@@ -126,7 +126,8 @@ def tile_list_crystal_disagreement_scores_kernel(
         nc.vector.memset(placed_last[:], 0)
 
         nc.sync.dma_start(offsets[:], offs)
-        nc.scalar.dma_start(tab_sc[2 * QUADRANT : 3 * QUADRANT, :], tab_scales[0:2].rearrange("g q n -> q g n").bitcast(I32))
+        for g in range(2):
+            nc.scalar.dma_start(tab_sc[2 * QUADRANT + g : 3 * QUADRANT : 2, :], tab_scales[g].bitcast(I32))
         nc.sync.dma_start(tab_sc[P - PASS_ROWS :, :], tab_scales[2].bitcast(I32))
         load_tab(0)
         for q in range(P // QUADRANT):
@@ -140,8 +141,8 @@ def tile_list_crystal_disagreement_scores_kernel(
         gather_words(0, 0, S)
         place_pair()
         load_tab(2)
-        place_last()
         load_w1(0)
+        place_last()
         load_w1(1)
         load_w1(2)
         g_rows = gT.rearrange("(p t) n -> p t n", t=PACK)

@@ -78,8 +78,8 @@ def tile_list_crystal_disagreement_scores_kernel(
         def listed(lo, hi):
             return offsets[:, lo // LIST_ROWS : hi // LIST_ROWS]
 
-        def load_tab(g):
-            nc.sync.dma_start(tab[g][:], tab_words[g].rearrange("p n i -> p (n i)").bitcast(I32))
+        def load_tab(g, lo=0, hi=T):
+            nc.sync.dma_start(tab[g][:, lo:hi], tab_words[g].rearrange("p n i -> p (n i)").bitcast(I32)[:, lo:hi])
 
         def place_pair():
             for q in range(P // QUADRANT):
@@ -96,6 +96,12 @@ def tile_list_crystal_disagreement_scores_kernel(
                     placed_last[QUADRANT * q : QUADRANT * q + SCALE_ROWS, :],
                     sc_rows[first : first + SCALE_ROWS, :].bitcast(I32),
                 )
+
+        def load_w2_scales(queue, q):
+            queue.dma_start(
+                w2_sc_raw[QUADRANT * q : QUADRANT * q + SCALE_ROWS, :, :],
+                w2_scales[:, SCALE_ROWS * q : SCALE_ROWS * (q + 1), :].rearrange("g s c -> s g c").bitcast(I32),
+            )
 
         def load_w1(g):
             rows = w1[g * P * PACK : (g + 1) * P * PACK, :]
@@ -130,17 +136,17 @@ def tile_list_crystal_disagreement_scores_kernel(
             nc.scalar.dma_start(tab_sc[2 * QUADRANT + g : 3 * QUADRANT : 2, :], tab_scales[g].bitcast(I32))
         nc.sync.dma_start(tab_sc[P - PASS_ROWS :, :], tab_scales[2].bitcast(I32))
         load_tab(0)
-        for q in range(P // QUADRANT):
-            nc.scalar.dma_start(
-                w2_sc_raw[QUADRANT * q : QUADRANT * q + SCALE_ROWS, :, :],
-                w2_scales[:, SCALE_ROWS * q : SCALE_ROWS * (q + 1), :].rearrange("g s c -> s g c").bitcast(I32),
-            )
+        load_w2_scales(nc.scalar, 0)
+        load_w2_scales(nc.scalar, 1)
         nc.sync.dma_start(w2_raw[:], w2_words.rearrange("g p c -> p g c").bitcast(I32))
+        load_w2_scales(nc.sync, 2)
+        load_w2_scales(nc.sync, 3)
         load_tab(1)
+        load_tab(2, 0, T // 4)
         nc.vector.tensor_copy(sc_rows[:], tab_sc[:].bitcast(U8).indirect(offsets[:]))
         gather_words(0, 0, S)
         place_pair()
-        load_tab(2)
+        load_tab(2, T // 4, T)
         load_w1(0)
         place_last()
         load_w1(1)

from contextlib import ExitStack

import concourse.mybir as mybir
from concourse.masks import make_identity

K, T, S, H, N = 1536, 2048, 1024, 512, 256
FLOPS = 2 * (2 * K * H * S + H * N * S)

F32 = mybir.dt.float32
BF16 = mybir.dt.bfloat16
I32 = mybir.dt.int32
U32 = mybir.dt.uint32
U16 = mybir.dt.uint16
U8 = mybir.dt.uint8
FP8X4 = mybir.dt.float8_e4m3fn_x4
FP4X4 = mybir.dt.float4_e2m1fn_x4
ACT = mybir.ActivationFunctionType
ALU = mybir.AluOpType

P = 128
PACK = 4
PASSES = K // (P * PACK)
QUADRANT = 32
SCALE_ROWS = 4
LIST_ROWS = 16
HALF = S // 2
CHUNK = 2 * P
TAIL = P // 2
RUN = 4
DMA_ALIGN = 256
PASS_ROWS = 16


def tile_list_crystal_disagreement_scores_kernel(
    tc, tab_words, tab_scales, offs, w1, w2_words, w2_scales, gT, w3, out
):
    nc = tc.nc
    with ExitStack() as ctx:
        keep = ctx.enter_context(tc.tile_pool(name="keep", bufs=1))
        psum = ctx.enter_context(tc.psum_pool(name="psum", bufs=1))

        offsets = keep.tile([P, S // LIST_ROWS], U16, name="offsets")
        tab = [keep.tile([P, T], I32, name=f"tab{g}", align_bytes=DMA_ALIGN) for g in range(PASSES)]
        w1_raw = [keep.tile([P, PACK, H], F32, name=f"w1_raw{g}", align_bytes=DMA_ALIGN) for g in range(PASSES)]
        g_tab = [keep.tile([P, T], F32, name=f"g_tab{t}", align_bytes=DMA_ALIGN) for t in range(PACK)]
        w3_raw = keep.tile([P, PACK, N], F32, name="w3_raw", align_bytes=DMA_ALIGN)
        tab_sc = keep.tile([P, T // 4], I32, name="tab_sc", align_bytes=DMA_ALIGN)
        w2_raw = keep.tile([P, PASSES, H // 2], I32, name="w2_raw", align_bytes=DMA_ALIGN)
        w2_sc_raw = keep.tile([P, PASSES, H // 4], I32, name="w2_sc_raw", align_bytes=DMA_ALIGN)

        v = [keep.tile([P, S], U32, name=f"v{g}", align_bytes=64) for g in range(PASSES)]
        sc_rows = keep.tile([P, S], U8, name="sc_rows", align_bytes=64)
        placed_pair = keep.tile([P, 2, S // 4], I32, name="placed_pair", align_bytes=64)
        placed_last = keep.tile([P, S // 4], I32, name="placed_last", align_bytes=64)
        v_sc = [placed_pair[:, 0, :].bitcast(U8), placed_pair[:, 1, :].bitcast(U8), placed_last[:].bitcast(U8)]
        w2q = keep.tile([P, PASSES, H // 2], I32, name="w2q", align_bytes=64)
        w2_sc = keep.tile([P, PASSES, H // 4], I32, name="w2_sc", align_bytes=64)
        w1_bf = [keep.tile([P, PACK * H], BF16, name=f"w1_bf{g}", align_bytes=64) for g in range(PASSES)]
        w1q = [keep.tile([P, H], U32, name=f"w1q{g}", align_bytes=64) for g in range(PASSES)]
        w1_sc = [keep.tile([P, H], U8, name=f"w1_sc{g}", align_bytes=64) for g in range(PASSES)]
        w3_bf = keep.tile([P, PACK * N], BF16, name="w3_bf", align_bytes=64)
        w3_sc = keep.tile([P, N], U8, name="w3_sc", align_bytes=64)

        h_first = keep.tile([P, PACK, HALF], F32, name="h_first")
        h_block = [keep.tile([P, PACK, P], F32, name=f"h_block{i}") for i in range(2)]
        h_of_block = (h_block[0], h_block[1], h_first, h_block[1])

        def h_f32(lo, hi):
            if lo < HALF:
                return h_first[:, :, lo:hi]
            j = (lo - HALF) // P
            return h_of_block[j][:, :, lo - HALF - j * P : hi - HALF - j * P]

        h_bf = keep.tile([P, S * PACK], BF16, name="h_bf", align_bytes=64)
        hq = keep.tile([P, S], U32, name="hq", align_bytes=64)
        h_sc = keep.tile([P, S], U8, name="h_sc", align_bytes=64)

        def listed(lo, hi):
            return offsets[:, lo // LIST_ROWS : hi // LIST_ROWS]

        def load_tab(g, lo=0, hi=T):
            nc.sync.dma_start(tab[g][:, lo:hi], tab_words[g].rearrange("p n i -> p (n i)").bitcast(I32)[:, lo:hi])

        def place_pair():
            for q in range(P // QUADRANT):
                first = 2 * QUADRANT + 2 * SCALE_ROWS * q
                nc.sync.dma_start(
                    placed_pair[QUADRANT * q : QUADRANT * q + SCALE_ROWS, :, :],
                    sc_rows[first : first + 2 * SCALE_ROWS, :].bitcast(I32),
                )

        def place_last():
            for q in range(P // QUADRANT):
                first = P - PASS_ROWS + SCALE_ROWS * q
                nc.sync.dma_start(
                    placed_last[QUADRANT * q : QUADRANT * q + SCALE_ROWS, :],
                    sc_rows[first : first + SCALE_ROWS, :].bitcast(I32),
                )

        def load_w2_scales(queue, q):
            queue.dma_start(
                w2_sc_raw[QUADRANT * q : QUADRANT * q + SCALE_ROWS, :, :],
                w2_scales[:, SCALE_ROWS * q : SCALE_ROWS * (q + 1), :].rearrange("g s c -> s g c").bitcast(I32),
            )

        def load_w1(g):
            rows = w1[g * P * PACK : (g + 1) * P * PACK, :]
            nc.sync.dma_start(w1_raw[g][:], rows.rearrange("(p i) c -> p i c", i=PACK))

        def gather_words(g, lo, hi):
            nc.vector.tensor_copy(v[g][:, lo:hi], tab[g][:].bitcast(U32).indirect(listed(lo, hi)))

        def interleave_w1(engine_copy, g, t0, t1):
            engine_copy(
                w1_bf[g][:].rearrange("p (t m i) -> p m i t", t=PACK, i=PACK)[:, :, :, t0:t1],
                w1_raw[g][:].rearrange("p i (m t) -> p m i t", t=PACK)[:, :, :, t0:t1],
            )

        def quantize_w1(g, t0, t1):
            nc.vector.quantize_mx(
                out=w1q[g][:, t0 * P : t1 * P].bitcast(FP8X4),
                scales=w1_sc[g][:, t0 * P : t1 * P],
                in_=w1_bf[g][:, t0 * P * PACK : t1 * P * PACK],
            )

        nc.gpsimd.memset(w2_sc_raw[:], 0)
        nc.vector.memset(tab_sc[0 : 2 * QUADRANT, :], 0)
        nc.vector.memset(tab_sc[3 * QUADRANT : 3 * QUADRANT + PASS_ROWS, :], 0)
        ident = keep.tile([P, P], F32, name="ident")
        make_identity(nc, ident[:])
        nc.vector.memset(placed_pair[:], 0)
        nc.vector.memset(placed_last[:], 0)

        nc.sync.dma_start(offsets[:], offs)
        for g in range(2):
            nc.scalar.dma_start(tab_sc[2 * QUADRANT + g : 3 * QUADRANT : 2, :], tab_scales[g].bitcast(I32))
        nc.sync.dma_start(tab_sc[P - PASS_ROWS :, :], tab_scales[2].bitcast(I32))
        load_tab(0)
        load_w2_scales(nc.scalar, 0)
        load_w2_scales(nc.scalar, 1)
        nc.sync.dma_start(w2_raw[:], w2_words.rearrange("g p c -> p g c").bitcast(I32))
        load_w2_scales(nc.sync, 2)
        load_w2_scales(nc.sync, 3)
        load_tab(1)
        load_tab(2, 0, T // 4)
        nc.vector.tensor_copy(sc_rows[:], tab_sc[:].bitcast(U8).indirect(offsets[:]))
        gather_words(0, 0, S)
        place_pair()
        load_tab(2, T // 4, T)
        load_w1(0)
        place_last()
        load_w1(1)
        load_w1(2)
        g_rows = gT.rearrange("(p t) n -> p t n", t=PACK)
        nc.sync.dma_start(w3_raw[:], w3.rearrange("(p t) n -> p t n", t=PACK))
        for t in range(PACK):
            nc.sync.dma_start(g_tab[t][:], g_rows[:, t, :])

        nc.scalar.copy(
            w2q[:].bitcast(U16).rearrange("p g (t m) -> p t g m", t=PACK),
            w2_raw[:].bitcast(U16).rearrange("p g (m t) -> p t g m", t=PACK),
        )
        nc.gpsimd.tensor_copy(
            w2_sc[:].bitcast(U8).rearrange("p g (t m) -> p t g m", t=PACK),
            w2_sc_raw[:].bitcast(U8).rearrange("p g (m t) -> p t g m", t=PACK),
        )
        for g in range(1, PASSES):
            gather_words(g, 0, HALF)
            gather_words(g, HALF, S)
        interleave_w1(nc.vector.tensor_copy, 0, 0, PACK // 2)
        interleave_w1(nc.vector.tensor_copy, 0, PACK // 2, PACK)
        quantize_w1(0, 0, PACK)
        for g in range(1, PASSES):
            interleave_w1(nc.vector.tensor_copy, g, 0, PACK // 2)
            interleave_w1(nc.vector.tensor_copy, g, PACK // 2, PACK)
            quantize_w1(g, 0, PACK // 2)
            quantize_w1(g, PACK // 2, PACK)

        tanh_a = [keep.tile([P, HALF], F32, name=f"tanh_a{u}") for u in range(2 * PACK)]
        tanh_b_first = keep.tile([P, PACK, HALF], F32, name="tanh_b_first")
        tanh_b = [tanh_b_first[:, t, :] for t in range(PACK)]
        tanh_b.extend(keep.tile([P, HALF], F32, name=f"tanh_b{u}")[:] for u in range(PACK))
        sq_first = [keep.tile([P, HALF], F32, name=f"sq{t}")[:] for t in range(2)]
        sq_first.extend(block[:].rearrange("p t c -> p (t c)") for block in h_block)
        sq_second = keep.tile([P, PACK, HALF], F32, name="sq_second")
        w3q = keep.tile([P, N], U32, name="w3q", align_bytes=64)

        banks = [psum.tile([P, HALF], F32, name=f"bank{i}") for i in range(2 * PACK)]
        block_b_bank = (4, 5, 6, 7)
        block_a_bank = (0, 1, 2, 3)
        difference_bank = (4, 5, 6, 7)

        def passes(bank, stationary, moving):
            for g in range(PASSES):
                nc.tensor.matmul_mx(
                    out=bank[:],
                    lhsT=stationary(g)[0],
                    lhsT_scale=stationary(g)[1],
                    rhs=moving(g)[0],
                    rhs_scale=moving(g)[1],
                    start=(g == 0),
                    stop=(g == PASSES - 1),
                )

        def tokens(lo, hi):
            return lambda g: (v[g][:, lo:hi].bitcast(FP8X4), v_sc[g][:, lo:hi])

        def w1_cols(lo, hi):
            return lambda g: (w1q[g][:, lo:hi].bitcast(FP8X4), w1_sc[g][:, lo:hi])

        def w2_cols(lo, hi):
            return lambda g: (
                w2q[:, g, :].bitcast(U8)[:, 2 * lo : 2 * hi].bitcast(FP4X4),
                w2_sc[:, g, :].bitcast(U8)[:, lo:hi],
            )

        def head_b(t):
            passes(banks[t], w2_cols(t * P, (t + 1) * P), tokens(0, HALF))
            nc.scalar.activation(tanh_b[t], banks[t][:], ACT.Tanh)

        def head_a(t):
            passes(banks[t], w1_cols(t * P, (t + 1) * P), tokens(0, HALF))
            nc.scalar.activation(tanh_a[t][:], banks[t][:], ACT.Tanh)

        def difference(t):
            nc.vector.tensor_tensor(sq_first[t], tanh_a[t][:], tanh_b[t], ALU.subtract)

        def square(t):
            nc.scalar.activation(sq_first[t], sq_first[t], ACT.Square)

        def block_b(j):
            bank = banks[block_b_bank[j]]
            passes(bank, tokens(HALF + j * P, HALF + (j + 1) * P), w2_cols(0, H))
            nc.scalar.activation(tanh_b[PACK + j], bank[:], ACT.Tanh, scale=-1.0)

        def block_a(j):
            bank = banks[block_a_bank[j]]
            passes(bank, tokens(HALF + j * P, HALF + (j + 1) * P), w1_cols(0, H))
            nc.scalar.activation(tanh_a[PACK + j][:], bank[:], ACT.Tanh)

        def block_square(j):
            bank = banks[difference_bank[j]]
            for t in range(PACK):
                cols = slice(t * P, (t + 1) * P)
                for values, first in ((tanh_a[PACK + j], True), (tanh_b[PACK + j], False)):
                    nc.tensor.matmul(
                        bank[:, cols], values[:, cols], ident[:], start=first, stop=not first, is_transpose=True
                    )
            nc.scalar.activation(
                sq_second[:, :, j * P : (j + 1) * P], bank[:].rearrange("p (t c) -> p t c", t=PACK), ACT.Square
            )

        def weigh(t, lo, hi):
            sq = sq_first[t][:, lo:hi] if lo < HALF else sq_second[:, t, lo - HALF : hi - HALF]
            nc.vector.tensor_tensor(h_f32(lo, hi)[:, t, :], g_tab[t][:].indirect(listed(lo, hi)), sq, ALU.mult)

        def interleave(engine_copy, words, planes):
            engine_copy(
                words.rearrange("p (c e t) -> p c t e", e=RUN, t=PACK), planes.rearrange("p t (c e) -> p c t e", e=RUN)
            )

        def interleave_h(engine_copy, lo, hi):
            interleave(engine_copy, h_bf[:, lo * PACK : hi * PACK], h_f32(lo, hi))

        out_view = out.rearrange("(b p) j -> p b j", p=P)

        def quantize_h(lo, hi):
            nc.vector.quantize_mx(
                out=hq[:, lo:hi].bitcast(FP8X4), scales=h_sc[:, lo:hi], in_=h_bf[:, lo * PACK : hi * PACK]
            )

        def read_out(bank_index, lo, hi, engine_copy, queue):
            bank = banks[bank_index][:, 0 : (N // P) * (hi - lo)].rearrange("p (b j) -> p b j", b=N // P)
            for b in range(N // P):
                nc.tensor.matmul_mx(
                    out=bank[:, b, :],
                    lhsT=w3q[:, b * P : (b + 1) * P].bitcast(FP8X4),
                    lhsT_scale=w3_sc[:, b * P : (b + 1) * P],
                    rhs=hq[:, lo:hi].bitcast(FP8X4),
                    rhs_scale=h_sc[:, lo:hi],
                    start=True,
                    stop=True,
                )
            res = keep.tile([P, N // P, hi - lo], F32, name=f"res{lo}", align_bytes=DMA_ALIGN)
            engine_copy(res[:], bank[:])
            queue.dma_start(out_view[:, :, lo:hi], res[:])

        def block_tokens(j):
            return HALF + j * P, HALF + (j + 1) * P

        def weigh_block(j):
            for t in range(PACK):
                weigh(t, *block_tokens(j))
            interleave_h(nc.scalar.copy, *block_tokens(j))

        for t in range(PACK):
            head_b(t)
        for j in range(PACK):
            block_b(j)
        for t in range(PACK):
            head_a(t)
        for t in range(PACK):
            difference(t)
        square(0)
        block_a(0)
        square(1)
        block_a(1)
        square(2)
        for t in range(PACK - 1):
            weigh(t, 0, HALF)
        block_square(0)
        block_square(1)
        square(PACK - 1)
        for j in (2, 3):
            block_a(j)
        block_square(2)
        interleave(nc.vector.tensor_copy, w3_bf[:], w3_raw[:])
        weigh(PACK - 1, 0, CHUNK)
        weigh(PACK - 1, CHUNK, HALF)
        nc.vector.quantize_mx(out=w3q[:].bitcast(FP8X4), scales=w3_sc[:], in_=w3_bf[:])
        interleave_h(nc.vector.tensor_copy, 0, P)
        interleave_h(nc.scalar.copy, P, CHUNK)
        block_square(3)
        interleave_h(nc.scalar.copy, CHUNK, HALF)
        weigh_block(0)
        weigh_block(1)
        quantize_h(0, CHUNK)
        read_out(0, 0, CHUNK, nc.scalar.copy, nc.sync)
        weigh_block(2)
        quantize_h(CHUNK, HALF)
        quantize_h(HALF, HALF + CHUNK)
        quantize_h(*block_tokens(2))
        read_out(1, CHUNK, HALF, nc.scalar.copy, nc.sync)
        read_out(2, HALF, HALF + CHUNK, nc.scalar.copy, nc.sync)
        tails = ((S - P, S - TAIL), (S - TAIL, S))
        for t in range(PACK - 1):
            weigh(t, S - P, S)
        for lo, hi in tails:
            weigh(PACK - 1, lo, hi)
        for lo, hi in tails:
            interleave_h(nc.vector.tensor_copy, lo, hi)
        for lo, hi in tails:
            quantize_h(lo, hi)
        read_out(3, *block_tokens(2), nc.scalar.copy, nc.sync)
        read_out(4, *tails[0], nc.scalar.copy, nc.sync)
        read_out(5, *tails[1], nc.vector.tensor_copy, nc.sync)
